import numpy as np
import ml_dtypes


def mxq(x, axis, fmt="e4m3"):
    dtype, down = {"e4m3": (ml_dtypes.float8_e4m3fn, 7), "e5m2": (ml_dtypes.float8_e5m2, 14)}[fmt]
    v = np.moveaxis(np.asarray(x, np.float32).astype(ml_dtypes.bfloat16).astype(np.float64), axis, -1)
    blocks = v.reshape(v.shape[:-1] + (-1, 32))
    amax = np.abs(blocks).max(-1, keepdims=True)
    byte = np.maximum(np.where(amax > 0, np.frexp(amax)[1] - 1 + 127, 0) - down, 1)
    scale = np.exp2(byte - 127.0)
    codes = (blocks / scale).astype(np.float32).astype(dtype).astype(np.float64)
    return np.moveaxis((codes * scale).reshape(v.shape), -1, axis)


WIDE = False


def mx_kscale(k):
    if not WIDE:
        return np.ones(k)
    levels = np.array([24, -24, 12, -12, 0])
    if k % 512:
        return np.exp2(np.random.permutation(np.resize(levels, k // 32))).repeat(32)
    a = np.empty((k // 512, 16))
    for p in range(k // 512):
        a[p, :8] = np.random.permutation(np.resize(levels, 8))
        for g in range(8):
            far = levels[np.abs(levels - a[p, g]) >= 10]
            a[p, g + 8] = far[np.random.randint(len(far))]
    return np.exp2(a.ravel()).repeat(32)


def f64(x):
    return np.asarray(x).astype(np.float64)


def striped(idx):
    return np.tile(idx.reshape(-1, 16).T, (8, 1)).astype(np.uint16)


def unstriped(offs):
    return offs[:16].T.reshape(-1).astype(np.int64)


E2M1 = np.array([0.0, 0.5, 1.0, 1.5, 2.0, 3.0, 4.0, 6.0, -0.0, -0.5, -1.0, -1.5, -2.0, -3.0, -4.0, -6.0])


def pack_weight(w, fmt):
    k, n = w.shape
    w = f64(np.asarray(w, np.float32).astype(ml_dtypes.bfloat16)).reshape(k // 32, 32, n)
    amax = np.abs(w).max(1)
    if fmt == "e4m3":
        byte = np.frexp(amax)[1] - 1 + 127 - 7
    else:
        mant, ex = np.frexp(amax / 6.0)
        byte = np.where(mant > 0.5, ex, ex - 1) + 127
    byte = np.clip(np.where(amax > 0, byte, 1), 1, 254)
    scaled = (w * np.exp2(127.0 - byte)[:, None, :]).reshape(k, n).astype(np.float32)
    by_word = np.ascontiguousarray(scaled.reshape(k // 512, 128, 4, n).transpose(0, 1, 3, 2))
    if fmt == "e4m3":
        words = by_word.astype(ml_dtypes.float8_e4m3fn).view(np.uint8)
    else:
        c = by_word.astype(ml_dtypes.float4_e2m1fn).view(np.uint8) & 0xF
        words = (c[..., 0::2] | (c[..., 1::2] << 4)).reshape(k // 512, 128, 2 * n)
    return np.ascontiguousarray(words), np.ascontiguousarray(byte.astype(np.uint8).reshape(k // 512, 16, n))


def unpack_weight(words, scales, fmt):
    g, _, n = scales.shape
    words = np.ascontiguousarray(words).reshape(g, 128, n, -1)
    if fmt == "e4m3":
        vals = words.view(ml_dtypes.float8_e4m3fn).astype(np.float64)
    else:
        nib = np.empty((g, 128, n, 4), np.uint8)
        nib[..., 0::2] = words & 0xF
        nib[..., 1::2] = words >> 4
        vals = E2M1[nib]
    vals = vals * np.repeat(np.exp2(scales.astype(np.float64) - 127.0), 8, axis=1)[..., None]
    return vals.transpose(0, 1, 3, 2).reshape(g * 512, n)


def pack_table4(v):
    words, scales = pack_weight(v, "e2m1")
    g, t = words.shape[0] // 2, v.shape[1]
    return np.ascontiguousarray(words.reshape(g, 2, 128, t, 2).transpose(0, 2, 3, 1, 4).reshape(g, 128, t, 4)), scales


def unpack_table4(words, scales):
    g, _, t, _ = words.shape
    return unpack_weight(words.reshape(g, 128, t, 2, 2).transpose(0, 3, 1, 2, 4).reshape(2 * g, 128, 2 * t), scales, "e2m1")


K, R, N, T, J = 1024, 1024, 512, 2048, 1024


def setup_inputs():
    n = np.random.standard_normal
    s = mx_kscale(K)[:, None]
    u = mx_kscale(R)[:, None]
    p_tab = pack_table4(n((K, T)) * s)
    p_wb = pack_weight(0.7 * n((K, N)) / np.sqrt(K) / s, "e2m1")
    p_dn = pack_weight(n((K, R)) / np.sqrt(K) / s * u.T, "e2m1")
    return {
        "tab_words": p_tab[0],
        "tab_scales": p_tab[1],
        "wb_words": p_wb[0],
        "wb_scales": p_wb[1],
        "dn_words": p_dn[0],
        "dn_scales": p_dn[1],
        "upw": (2.0 * n((R, N)) / np.sqrt(R) / u).astype(np.float32),
        "x0T": (n((N, T))).astype(np.float32),
        "b": (0.3 * n(N)).astype(np.float32),
        "offs": striped(np.random.permutation(T)[:J]),
    }


def reference(tab_words, tab_scales, wb_words, wb_scales, dn_words, dn_scales, upw, x0T, b, offs):
    idx = unstriped(offs)
    tab_ = unpack_table4(tab_words, tab_scales)[:, idx]
    wb_ = unpack_weight(wb_words, wb_scales, "e2m1")
    dn_ = unpack_weight(dn_words, dn_scales, "e2m1")
    hs = dn_.T @ tab_
    h = hs
    h_ = mxq(h, 0, "e4m3")
    upw_ = mxq(f64(upw), 0, "e4m3")
    y = wb_.T @ tab_ + upw_.T @ h_
    return f64(x0T)[:, idx] * (y + f64(b)[:, None]) + f64(x0T)[:, idx]

@@ -1,0 +1,228 @@
+from contextlib import ExitStack
+
+import concourse.mybir as mybir
+
+K, R, N, T, J = 1024, 1024, 512, 2048, 1024
+FLOPS = 2 * J * (K * R + K * N + R * N)
+
+F32 = mybir.dt.float32
+BF16 = mybir.dt.bfloat16
+I32 = mybir.dt.int32
+U32 = mybir.dt.uint32
+U16 = mybir.dt.uint16
+U8 = mybir.dt.uint8
+FP8X4 = mybir.dt.float8_e4m3fn_x4
+FP4X4 = mybir.dt.float4_e2m1fn_x4
+ADD = mybir.AluOpType.add
+MULT = mybir.AluOpType.mult
+
+P = 128
+HALF = 512
+CH = 128
+
+
+def tile_list_xcross_none_kernel(
+    tc, tab_words, tab_scales, wb_words, wb_scales, dn_words, dn_scales, upw, x0T, b, offs, out
+):
+    nc = tc.nc
+    with ExitStack() as ctx:
+        keep = ctx.enter_context(tc.tile_pool(name="keep", bufs=1))
+        shared = ctx.enter_context(tc.tile_pool(name="shared", bufs=1))
+        res = ctx.enter_context(tc.tile_pool(name="res", bufs=4))
+        ps_h = ctx.enter_context(tc.psum_pool(name="ps_h", bufs=4))
+        ps_y = ctx.enter_context(tc.psum_pool(name="ps_y", bufs=4))
+
+        def kt(shape, dt, name):
+            return keep.tile(shape, dt, name=name, align_bytes=64)
+
+        def st(shape, dt, name, offset):
+            return shared.tile(shape, dt, name=name, align_bytes=64, offset=offset)
+
+        lst = keep.tile([P, J // 16], U16, name="lst")
+        ts = kt([P, T], U8, "ts")
+        tw = kt([P, T], U32, "tw")
+        ws = kt([P, 2, N // 4], I32, "ws")
+        bias1 = kt([P, 4], F32, "bias1")
+        sh = [kt([P, HALF], U8, f"sh{h}") for h in range(2)]
+        tp = [kt([P, 2, HALF], U16, f"tp{h}") for h in range(2)]
+        dw = [kt([P, 2, 256], I32, f"dw{g}") for g in range(2)]
+        ds = [kt([P, 2, 128], I32, f"ds{g}") for g in range(2)]
+        up_bf = [kt([P, N, 4], BF16, f"up_bf{g}") for g in range(2)]
+        up_c = [kt([P, N], U32, f"up_c{g}") for g in range(2)]
+        up_s = [kt([P, N], U8, f"up_s{g}") for g in range(2)]
+        hb = [[kt([P, HALF, 4], BF16, f"hb{h}_{g}") for g in range(2)] for h in range(2)]
+        hc = [[kt([P, HALF], U32, f"hc{h}_{g}") for g in range(2)] for h in range(2)]
+        hs = [[kt([P, HALF], U8, f"hs{h}_{g}") for g in range(2)] for h in range(2)]
+
+        KB = 1024
+        ww = st([P, 2, N // 2], I32, "ww", 0)
+        up_raw = [st([P, 4, N], F32, "up_raw0", 2 * KB), st([P, 4, N], F32, "up_raw1", 31 * KB)]
+        xs = [st([P, T], F32, f"xs{c}", at * KB) for c, at in enumerate((39, 10, 22, 39))]
+        xg = [st([P, J], F32, "xg0", 18 * KB)] + [kt([P, J], F32, f"xg{c}") for c in range(1, 4)]
+        gw = [st([P, HALF], U32, "gw0", 1 * KB), st([P, HALF], U32, "gw1", 18 * KB)]
+        dw_raw = st([P, 2, R // 2], I32, "dw_raw", 17 * KB)
+        ds_raw = st([P, 2, R // 4], I32, "ds_raw", 29 * KB + 512)
+        gs = [kt([P, HALF], U8, "gs0"), st([P, HALF], U8, "gs1", 30 * KB)]
+        bias = st([P, 4], F32, "bias", 30 * KB + 512)
+
+        nc.gpsimd.memset(ts[:].bitcast(I32), 0)
+        nc.vector.memset(ds_raw[:], 0)
+        for h in range(2):
+            nc.vector.memset(sh[h][:].bitcast(I32), 0)
+        nc.vector.memset(ws[:], 0)
+
+        nc.sync.dma_start(lst[:], offs)
+        nc.sync.dma_start(tw[:].bitcast(I32), tab_words[0].rearrange("p t b -> p (t b)").bitcast(I32))
+        ts_src = tab_scales.bitcast(I32).rearrange("a (q r) c -> r q a c", r=4)
+        for r in range(4):
+            nc.scalar.dma_start(ts[:].bitcast(I32)[r:P:16, :], ts_src[r])
+        nc.sync.dma_start(dw_raw[:], dn_words.bitcast(I32).rearrange("a p c -> p a c"))
+        ds_src = dn_scales.bitcast(I32).rearrange("a q c -> q a c")
+        for q in range(4):
+            nc.gpsimd.dma_start(ds_raw[32 * q : 32 * q + 4], ds_src[4 * q : 4 * q + 4])
+        nc.sync.dma_start(xs[0][:], x0T[0:P, :])
+        ws_src = wb_scales.bitcast(I32).rearrange("a q c -> q a c")
+        for q in range(4):
+            nc.scalar.dma_start(ws[32 * q : 32 * q + 4], ws_src[4 * q : 4 * q + 4])
+        up_src = upw.rearrange("(g u t i) n -> g t u i n", g=2, t=4, i=8)
+
+        def load_up(g):
+            for t in range(4):
+                nc.sync.dma_start(up_raw[g][:, t, :], up_src[g][t])
+
+        def load_x(c):
+            nc.sync.dma_start(xs[c][:], x0T[P * c : P * (c + 1), :])
+
+        def part_of_list(h):
+            return lst[:, 32 * h : 32 * (h + 1)]
+
+        def gather_scales(h):
+            nc.vector.tensor_copy(gs[h][:], ts[:].indirect(part_of_list(h)))
+            nc.gpsimd.dma_start(sh[h][:].bitcast(I32)[0:112, :], gs[h][:].bitcast(I32)[16:128, :])
+
+        def gather_words(h):
+            nc.vector.tensor_copy(gw[h][:], tw[:].indirect(part_of_list(h)))
+            nc.vector.tensor_copy(tp[h][:], gw[h][:].bitcast(U16).rearrange("p (j d) -> p d j", d=2))
+
+        def deal_dn(g):
+            nc.vector.tensor_copy(
+                dw[g][:].rearrange("p a (t u w) -> p a t u w", t=4, w=4),
+                dw_raw[:, :, 256 * g : 256 * (g + 1)].rearrange("p a (u t w) -> p a t u w", t=4, w=4),
+            )
+            nc.vector.tensor_copy(
+                ds[g][:].rearrange("p a (t u w) -> p a t u w", t=4, w=2),
+                ds_raw[:, :, 128 * g : 128 * (g + 1)].rearrange("p a (u t w) -> p a t u w", t=4, w=2),
+            )
+
+        def tab_operand(h, a, cols):
+            plane = (gs, sh)[a][h]
+            return dict(rhs=tp[h][:, a, cols].bitcast(FP4X4), rhs_scale=plane[:, cols])
+
+        def h_chunk(h, g, c):
+            bank = ps_h.tile([P, 4, CH], F32, name="bank")
+            cols = slice(CH * c, CH * (c + 1))
+            for t in range(4):
+                for a in range(2):
+                    nc.tensor.matmul_mx(
+                        out=bank[:, t, :],
+                        lhsT=dw[g][:, a, 64 * t : 64 * (t + 1)].bitcast(FP4X4),
+                        lhsT_scale=ds[g][:, a, 32 * t : 32 * (t + 1)].bitcast(U8),
+                        start=(a == 0),
+                        stop=(a == 1),
+                        **tab_operand(h, a, cols),
+                    )
+            nc.scalar.copy(hb[h][g][:, cols, :], bank[:].rearrange("p t j -> p j t"))
+
+        def quant_h(h, g):
+            nc.vector.quantize_mx(
+                out=hc[h][g][:].bitcast(FP8X4), scales=hs[h][g][:], in_=hb[h][g][:].rearrange("p j t -> p (j t)")
+            )
+
+        def cast_up(g, copy, lo, hi):
+            copy(
+                up_bf[g][:, lo:hi, :].rearrange("p (c i) t -> p c t i", i=4),
+                up_raw[g][:, :, lo:hi].rearrange("p t (c i) -> p c t i", i=4),
+            )
+
+        def quant_up(g):
+            nc.vector.quantize_mx(
+                out=up_c[g][:].bitcast(FP8X4), scales=up_s[g][:], in_=up_bf[g][:].rearrange("p n t -> p (n t)")
+            )
+
+        def y_wb(acc, h, c):
+            for a in range(2):
+                nc.tensor.matmul_mx(
+                    out=acc[:],
+                    lhsT=ww[:, a, 64 * c : 64 * (c + 1)].bitcast(FP4X4),
+                    lhsT_scale=ws[:, a, 32 * c : 32 * (c + 1)].bitcast(U8),
+                    start=(a == 0),
+                    stop=False,
+                    **tab_operand(h, a, slice(0, HALF)),
+                )
+
+        def y_up(acc, h, c, g):
+            cols = slice(P * c, P * (c + 1))
+            nc.tensor.matmul_mx(
+                out=acc[:],
+                lhsT=up_c[g][:, cols].bitcast(FP8X4),
+                lhsT_scale=up_s[g][:, cols],
+                rhs=hc[h][g][:].bitcast(FP8X4),
+                rhs_scale=hs[h][g][:],
+                start=False,
+                stop=(g == 1),
+            )
+
+        def gather_x(c):
+            nc.vector.tensor_copy(xg[c][:], xs[c][:].indirect(lst[:]))
+
+        def finish(acc, h, c):
+            o = res.tile([P, HALF], F32, name="o")
+            nc.vector.scalar_tensor_tensor(o[:], acc[:], bias1[:, c : c + 1], xg[c][:, HALF * h : HALF * (h + 1)], ADD, MULT)
+            nc.sync.dma_start(out[P * c : P * (c + 1), HALF * h : HALF * (h + 1)], o[:])
+
+        gather_scales(0)
+        gather_words(0)
+        deal_dn(0)
+        deal_dn(1)
+        nc.sync.dma_start(ww[:], wb_words.bitcast(I32).rearrange("a p c -> p a c"))
+        load_up(0)
+        load_x(1)
+        load_up(1)
+        with nc.allow_non_contiguous_dma(reason="one bias value a partition"):
+            nc.sync.dma_start(bias[:], b.rearrange("(c p) -> p c", p=P))
+        load_x(2)
+        gather_scales(1)
+        gather_words(1)
+        gather_x(0)
+        load_x(3)
+        nc.gpsimd.tensor_scalar_add(bias1[:], bias[:], 1.0)
+
+        acc0 = [ps_y.tile([P, HALF], F32, name="acc") for c in range(4)]
+        for g in range(2):
+            for c in range(4):
+                h_chunk(0, g, c)
+                if g == 1:
+                    y_wb(acc0[c], 0, c)
+                    cast_up(0, nc.scalar.copy, P * c, P * (c + 1))
+            quant_h(0, g)
+        quant_up(0)
+        for g in range(2):
+            for c in range(4):
+                h_chunk(1, g, c)
+                if g == 0:
+                    cast_up(1, nc.scalar.copy, P * c, P * (c + 1))
+            if g == 0:
+                quant_up(1)
+            quant_h(1, g)
+        for c in range(1, 4):
+            gather_x(c)
+        for c in range(4):
+            for g in range(2):
+                y_up(acc0[c], 0, c, g)
+            finish(acc0[c], 0, c)
+        for c in range(4):
+            acc = ps_h.tile([P, HALF], F32, name="bank")
+            y_wb(acc, 1, c)
+            for g in range(2):
+                y_up(acc, 1, c, g)
+            finish(acc, 1, c)

@@ -28,7 +28,6 @@ def tile_list_xcross_none_kernel(
     with ExitStack() as ctx:
         keep = ctx.enter_context(tc.tile_pool(name="keep", bufs=1))
         shared = ctx.enter_context(tc.tile_pool(name="shared", bufs=1))
-        res = ctx.enter_context(tc.tile_pool(name="res", bufs=4))
         ps_h = ctx.enter_context(tc.psum_pool(name="ps_h", bufs=4))
         ps_y = ctx.enter_context(tc.psum_pool(name="ps_y", bufs=4))
 
@@ -39,51 +38,55 @@ def tile_list_xcross_none_kernel(
             return shared.tile(shape, dt, name=name, align_bytes=64, offset=offset)
 
         lst = keep.tile([P, J // 16], U16, name="lst")
-        ts = kt([P, T], U8, "ts")
-        tw = kt([P, T], U32, "tw")
-        ws = kt([P, 2, N // 4], I32, "ws")
         bias1 = kt([P, 4], F32, "bias1")
-        sh = [kt([P, HALF], U8, f"sh{h}") for h in range(2)]
-        tp = [kt([P, 2, HALF], U16, f"tp{h}") for h in range(2)]
+        gs = kt([P, J], U8, "gs")
+        sh = kt([P, J], U8, "sh")
+        tp = [kt([P, 2 * HALF], U16, f"tp{h}") for h in range(2)]
         dw = [kt([P, 2, 256], I32, f"dw{g}") for g in range(2)]
         ds = [kt([P, 2, 128], I32, f"ds{g}") for g in range(2)]
         up_bf = [kt([P, N, 4], BF16, f"up_bf{g}") for g in range(2)]
         up_c = [kt([P, N], U32, f"up_c{g}") for g in range(2)]
         up_s = [kt([P, N], U8, f"up_s{g}") for g in range(2)]
         hb = [[kt([P, HALF, 4], BF16, f"hb{h}_{g}") for g in range(2)] for h in range(2)]
-        hc = [[kt([P, HALF], U32, f"hc{h}_{g}") for g in range(2)] for h in range(2)]
         hs = [[kt([P, HALF], U8, f"hs{h}_{g}") for g in range(2)] for h in range(2)]
 
         KB = 1024
-        ww = st([P, 2, N // 2], I32, "ww", 0)
-        up_raw = [st([P, 4, N], F32, "up_raw0", 2 * KB), st([P, 4, N], F32, "up_raw1", 31 * KB)]
-        xs = [st([P, T], F32, f"xs{c}", at * KB) for c, at in enumerate((39, 10, 22, 39))]
-        xg = [st([P, J], F32, "xg0", 18 * KB)] + [kt([P, J], F32, f"xg{c}") for c in range(1, 4)]
-        gw = [st([P, HALF], U32, "gw0", 1 * KB), st([P, HALF], U32, "gw1", 18 * KB)]
-        dw_raw = st([P, 2, R // 2], I32, "dw_raw", 17 * KB)
-        ds_raw = st([P, 2, R // 4], I32, "ds_raw", 29 * KB + 512)
-        gs = [kt([P, HALF], U8, "gs0"), st([P, HALF], U8, "gs1", 30 * KB)]
-        bias = st([P, 4], F32, "bias", 30 * KB + 512)
+        zeros = st([P, 1056], I32, "zeros", 8 * KB - 64)
+        tw = st([P, T], U32, "tw", 0)
+        dw_raw = st([P, 2, R // 2], I32, "dw_raw", 8 * KB)
+        ts = st([P, T], U8, "ts", 21 * KB + 512)
+        ds_raw = st([P, 2, R // 4], I32, "ds_raw", 38 * KB)
+        ww = st([P, 2, N // 2], I32, "ww", 20 * KB)
+        bias = st([P, 4], F32, "bias", 22 * KB)
+        ws = st([P, 2, N // 4], I32, "ws", 47 * KB)
+        up_raw = [st([P, 4, N], F32, "up_raw0", 12 * KB), st([P, 4, N], F32, "up_raw1", 31 * KB)]
+        xs = [st([P, T], F32, f"xs{c}", at * KB) for c, at in enumerate((23, 39, 0, 12))]
+        xg = [st([P, J], F32, "xg0", 8 * KB)] + [kt([P, J], F32, f"xg{c}") for c in range(1, 4)]
+        pieces = [(0, 256), (256, 512), (512, 1024)]
+        gw = [st([P, hi - lo], U32, f"gw{i}", at * KB) for i, ((lo, hi), at) in enumerate(zip(pieces, (47, 8, 9)))]
+        hc = [
+            [kt([P, HALF], U32, f"hc0_{g}") for g in range(2)],
+            [st([P, HALF], U32, "hc1_0", 0), st([P, HALF], U32, "hc1_1", 12 * KB)],
+        ]
+        res = [
+            [st([P, HALF], F32, f"o0_{c}", at * KB) for c, at in enumerate((2, 4, 6, 14))],
+            [kt([P, HALF], F32, f"o1_{c}") for c in range(4)],
+        ]
 
         nc.gpsimd.memset(ts[:].bitcast(I32), 0)
+        nc.vector.memset(zeros[:, 0:256], 0)
+        nc.vector.tensor_copy(sh[:].bitcast(I32), zeros[:, 0:256])
         nc.vector.memset(ds_raw[:], 0)
-        for h in range(2):
-            nc.vector.memset(sh[h][:].bitcast(I32), 0)
-        nc.vector.memset(ws[:], 0)
 
         nc.sync.dma_start(lst[:], offs)
-        nc.sync.dma_start(tw[:].bitcast(I32), tab_words[0].rearrange("p t b -> p (t b)").bitcast(I32))
         ts_src = tab_scales.bitcast(I32).rearrange("a (q r) c -> r q a c", r=4)
         for r in range(4):
-            nc.scalar.dma_start(ts[:].bitcast(I32)[r:P:16, :], ts_src[r])
-        nc.sync.dma_start(dw_raw[:], dn_words.bitcast(I32).rearrange("a p c -> p a c"))
+            nc.sync.dma_start(ts[:].bitcast(I32)[r:P:16, :], ts_src[r])
+        nc.sync.dma_start(tw[:].bitcast(I32), tab_words[0].rearrange("p t b -> p (t b)").bitcast(I32))
         ds_src = dn_scales.bitcast(I32).rearrange("a q c -> q a c")
         for q in range(4):
-            nc.gpsimd.dma_start(ds_raw[32 * q : 32 * q + 4], ds_src[4 * q : 4 * q + 4])
-        nc.sync.dma_start(xs[0][:], x0T[0:P, :])
-        ws_src = wb_scales.bitcast(I32).rearrange("a q c -> q a c")
-        for q in range(4):
-            nc.scalar.dma_start(ws[32 * q : 32 * q + 4], ws_src[4 * q : 4 * q + 4])
+            nc.sync.dma_start(ds_raw[32 * q : 32 * q + 4], ds_src[4 * q : 4 * q + 4])
+        nc.sync.dma_start(dw_raw[:], dn_words.bitcast(I32).rearrange("a p c -> p a c"))
         up_src = upw.rearrange("(g u t i) n -> g t u i n", g=2, t=4, i=8)
 
         def load_up(g):
@@ -93,16 +96,16 @@ def tile_list_xcross_none_kernel(
         def load_x(c):
             nc.sync.dma_start(xs[c][:], x0T[P * c : P * (c + 1), :])
 
-        def part_of_list(h):
-            return lst[:, 32 * h : 32 * (h + 1)]
+        def gather_scales(lo, hi):
+            nc.vector.tensor_copy(gs[:, lo:hi], ts[:].indirect(lst[:, lo // 16 : hi // 16]))
+            words = slice(lo // 4, hi // 4)
+            nc.scalar.dma_start(sh[:].bitcast(I32)[0:112, words], gs[:].bitcast(I32)[16:128, words])
 
-        def gather_scales(h):
-            nc.vector.tensor_copy(gs[h][:], ts[:].indirect(part_of_list(h)))
-            nc.gpsimd.dma_start(sh[h][:].bitcast(I32)[0:112, :], gs[h][:].bitcast(I32)[16:128, :])
-
-        def gather_words(h):
-            nc.vector.tensor_copy(gw[h][:], tw[:].indirect(part_of_list(h)))
-            nc.vector.tensor_copy(tp[h][:], gw[h][:].bitcast(U16).rearrange("p (j d) -> p d j", d=2))
+        def gather_words(i):
+            lo, hi = pieces[i]
+            nc.vector.tensor_copy(gw[i][:], tw[:].indirect(lst[:, lo // 16 : hi // 16]))
+            parted = tp[lo // HALF][:].rearrange("p (d j) -> p d j", d=2)[:, :, lo % HALF : lo % HALF + hi - lo]
+            nc.vector.tensor_copy(parted, gw[i][:].bitcast(U16).rearrange("p (j d) -> p d j", d=2))
 
         def deal_dn(g):
             nc.vector.tensor_copy(
@@ -115,8 +118,8 @@ def tile_list_xcross_none_kernel(
             )
 
         def tab_operand(h, a, cols):
-            plane = (gs, sh)[a][h]
-            return dict(rhs=tp[h][:, a, cols].bitcast(FP4X4), rhs_scale=plane[:, cols])
+            plane = (gs, sh)[a][:, HALF * h : HALF * (h + 1)]
+            return dict(rhs=tp[h][:, HALF * a : HALF * (a + 1)][:, cols].bitcast(FP4X4), rhs_scale=plane[:, cols])
 
         def h_chunk(h, g, c):
             bank = ps_h.tile([P, 4, CH], F32, name="bank")
@@ -176,49 +179,60 @@ def tile_list_xcross_none_kernel(
             nc.vector.tensor_copy(xg[c][:], xs[c][:].indirect(lst[:]))
 
         def finish(acc, h, c):
-            o = res.tile([P, HALF], F32, name="o")
+            o = res[h][c]
             nc.vector.scalar_tensor_tensor(o[:], acc[:], bias1[:, c : c + 1], xg[c][:, HALF * h : HALF * (h + 1)], ADD, MULT)
             nc.sync.dma_start(out[P * c : P * (c + 1), HALF * h : HALF * (h + 1)], o[:])
 
-        gather_scales(0)
+        load_up(0)
+        gather_scales(0, 256)
+        gather_scales(256, J)
         gather_words(0)
         deal_dn(0)
         deal_dn(1)
         nc.sync.dma_start(ww[:], wb_words.bitcast(I32).rearrange("a p c -> p a c"))
-        load_up(0)
-        load_x(1)
-        load_up(1)
+        load_x(0)
+        nc.gpsimd.memset(ws[:], 0)
+        ws_src = wb_scales.bitcast(I32).rearrange("a q c -> q a c")
+        for q in range(4):
+            nc.sync.dma_start(ws[32 * q : 32 * q + 4], ws_src[4 * q : 4 * q + 4])
         with nc.allow_non_contiguous_dma(reason="one bias value a partition"):
             nc.sync.dma_start(bias[:], b.rearrange("(c p) -> p c", p=P))
-        load_x(2)
-        gather_scales(1)
+        load_up(1)
+        load_x(1)
         gather_words(1)
-        gather_x(0)
+        gather_words(2)
+        load_x(2)
+        cast_up(0, nc.vector.tensor_copy, 0, N)
         load_x(3)
-        nc.gpsimd.tensor_scalar_add(bias1[:], bias[:], 1.0)
+        quant_up(0)
+        gather_x(0)
+        nc.vector.tensor_scalar_add(bias1[:], bias[:], 1.0)
 
         acc0 = [ps_y.tile([P, HALF], F32, name="acc") for c in range(4)]
-        for g in range(2):
-            for c in range(4):
-                h_chunk(0, g, c)
-                if g == 1:
-                    y_wb(acc0[c], 0, c)
-                    cast_up(0, nc.scalar.copy, P * c, P * (c + 1))
-            quant_h(0, g)
-        quant_up(0)
-        for g in range(2):
-            for c in range(4):
-                h_chunk(1, g, c)
-                if g == 0:
-                    cast_up(1, nc.scalar.copy, P * c, P * (c + 1))
-            if g == 0:
-                quant_up(1)
-            quant_h(1, g)
-        for c in range(1, 4):
-            gather_x(c)
+        for c0 in (0, 2):
+            for g in range(2):
+                for c in (c0, c0 + 1):
+                    h_chunk(0, g, c)
+                    if c0 == 2:
+                        y_wb(acc0[2 * g + c - 2], 0, 2 * g + c - 2)
+        quant_h(0, 0)
+        quant_h(0, 1)
+        cast_up(1, nc.scalar.copy, 0, N // 2)
+        cast_up(1, nc.scalar.copy, N // 2, N)
+        gather_x(1)
+        quant_up(1)
+        for c in range(4):
+            h_chunk(1, 0, c)
+        gather_x(2)
+        quant_h(1, 0)
         for c in range(4):
             for g in range(2):
                 y_up(acc0[c], 0, c, g)
+        for c in range(4):
+            h_chunk(1, 1, c)
+        gather_x(3)
+        quant_h(1, 1)
+        for c in range(4):
             finish(acc0[c], 0, c)
         for c in range(4):
             acc = ps_h.tile([P, HALF], F32, name="bank")

@@ -1,6 +1,7 @@
 from contextlib import ExitStack
 
 import concourse.mybir as mybir
+from concourse.masks import make_identity
 
 K, R, N, T, J = 1024, 1024, 512, 2048, 1024
 FLOPS = 2 * J * (K * R + K * N + R * N)
@@ -45,9 +46,7 @@ def tile_list_xcross_none_kernel(
         dw = [kt([P, 2, 256], I32, f"dw{g}") for g in range(2)]
         ds = [kt([P, 2, 128], I32, f"ds{g}") for g in range(2)]
         up_bf = [kt([P, N, 4], BF16, f"up_bf{g}") for g in range(2)]
-        up_c = [kt([P, N], U32, f"up_c{g}") for g in range(2)]
         up_s = [kt([P, N], U8, f"up_s{g}") for g in range(2)]
-        hb = [[kt([P, HALF, 4], BF16, f"hb{h}_{g}") for g in range(2)] for h in range(2)]
         hs = [[kt([P, HALF], U8, f"hs{h}_{g}") for g in range(2)] for h in range(2)]
 
         KB = 1024
@@ -57,23 +56,31 @@ def tile_list_xcross_none_kernel(
         ts = st([P, T], U8, "ts", 21 * KB + 512)
         ds_raw = st([P, 2, R // 4], I32, "ds_raw", 38 * KB)
         ww = st([P, 2, N // 2], I32, "ww", 20 * KB)
-        bias = st([P, 4], F32, "bias", 22 * KB)
+        bias = kt([P, P], F32, "bias")
+        ident = kt([P, P], F32, "ident")
         ws = st([P, 2, N // 4], I32, "ws", 47 * KB)
         up_raw = [st([P, 4, N], F32, "up_raw0", 12 * KB), st([P, 4, N], F32, "up_raw1", 31 * KB)]
         xs = [st([P, T], F32, f"xs{c}", at * KB) for c, at in enumerate((23, 39, 0, 12))]
         xg = [st([P, J], F32, "xg0", 8 * KB)] + [kt([P, J], F32, f"xg{c}") for c in range(1, 4)]
         pieces = [(0, 256), (256, 512), (512, 1024)]
         gw = [st([P, hi - lo], U32, f"gw{i}", at * KB) for i, ((lo, hi), at) in enumerate(zip(pieces, (47, 8, 9)))]
+        hb = [
+            [kt([P, HALF, 4], BF16, f"hb0_{g}") for g in range(2)],
+            [kt([P, HALF, 4], BF16, "hb1_0"), st([P, HALF, 4], BF16, "hb1_1", 48 * KB)],
+        ]
+        up_c = [kt([P, N], U32, "up_c0"), st([P, N], U32, "up_c1", 41 * KB)]
         hc = [
             [kt([P, HALF], U32, f"hc0_{g}") for g in range(2)],
             [st([P, HALF], U32, "hc1_0", 0), st([P, HALF], U32, "hc1_1", 12 * KB)],
         ]
         res = [
-            [st([P, HALF], F32, f"o0_{c}", at * KB) for c, at in enumerate((2, 4, 6, 14))],
+            [st([P, HALF], F32, f"o0_{c}", at * KB) for c, at in enumerate((2, 4, 48, 50))],
             [kt([P, HALF], F32, f"o1_{c}") for c in range(4)],
         ]
 
         nc.gpsimd.memset(ts[:].bitcast(I32), 0)
+        nc.gpsimd.memset(bias[:], 0.0)
+        make_identity(nc, ident[:])
         nc.vector.memset(zeros[:, 0:256], 0)
         nc.vector.tensor_copy(sh[:].bitcast(I32), zeros[:, 0:256])
         nc.vector.memset(ds_raw[:], 0)
@@ -87,6 +94,10 @@ def tile_list_xcross_none_kernel(
         for q in range(4):
             nc.sync.dma_start(ds_raw[32 * q : 32 * q + 4], ds_src[4 * q : 4 * q + 4])
         nc.sync.dma_start(dw_raw[:], dn_words.bitcast(I32).rearrange("a p c -> p a c"))
+        nc.scalar.dma_start(bias[0:4, :], b.rearrange("(c p) -> c p", p=P))
+        turned = ps_h.tile([P, P], F32, name="bank")
+        nc.tensor.transpose(turned[:], bias[:], ident[:])
+        nc.scalar.activation(bias1[:], turned[:, 0:4], mybir.ActivationFunctionType.Copy, bias=1.0)
         up_src = upw.rearrange("(g u t i) n -> g t u i n", g=2, t=4, i=8)
 
         def load_up(g):
@@ -134,7 +145,10 @@ def tile_list_xcross_none_kernel(
                         stop=(a == 1),
                         **tab_operand(h, a, cols),
                     )
-            nc.scalar.copy(hb[h][g][:, cols, :], bank[:].rearrange("p t j -> p j t"))
+            nc.scalar.copy(
+                hb[h][g][:, cols, :].rearrange("p (c i) t -> p c t i", i=2),
+                bank[:].rearrange("p t (c i) -> p c t i", i=2),
+            )
 
         def quant_h(h, g):
             nc.vector.quantize_mx(
@@ -178,10 +192,11 @@ def tile_list_xcross_none_kernel(
         def gather_x(c):
             nc.vector.tensor_copy(xg[c][:], xs[c][:].indirect(lst[:]))
 
-        def finish(acc, h, c):
-            o = res[h][c]
-            nc.vector.scalar_tensor_tensor(o[:], acc[:], bias1[:, c : c + 1], xg[c][:, HALF * h : HALF * (h + 1)], ADD, MULT)
-            nc.sync.dma_start(out[P * c : P * (c + 1), HALF * h : HALF * (h + 1)], o[:])
+        def finish(acc, h, c, lo=0, hi=HALF):
+            o = res[h][c][:, lo:hi]
+            cols = slice(HALF * h + lo, HALF * h + hi)
+            nc.vector.scalar_tensor_tensor(o, acc[:, lo:hi], bias1[:, c : c + 1], xg[c][:, cols], ADD, MULT)
+            nc.sync.dma_start(out[P * c : P * (c + 1), cols], o)
 
         load_up(0)
         gather_scales(0, 256)
@@ -189,14 +204,12 @@ def tile_list_xcross_none_kernel(
         gather_words(0)
         deal_dn(0)
         deal_dn(1)
-        nc.sync.dma_start(ww[:], wb_words.bitcast(I32).rearrange("a p c -> p a c"))
         load_x(0)
+        nc.sync.dma_start(ww[:], wb_words.bitcast(I32).rearrange("a p c -> p a c"))
         nc.gpsimd.memset(ws[:], 0)
         ws_src = wb_scales.bitcast(I32).rearrange("a q c -> q a c")
         for q in range(4):
             nc.sync.dma_start(ws[32 * q : 32 * q + 4], ws_src[4 * q : 4 * q + 4])
-        with nc.allow_non_contiguous_dma(reason="one bias value a partition"):
-            nc.sync.dma_start(bias[:], b.rearrange("(c p) -> p c", p=P))
         load_up(1)
         load_x(1)
         gather_words(1)
@@ -206,7 +219,6 @@ def tile_list_xcross_none_kernel(
         load_x(3)
         quant_up(0)
         gather_x(0)
-        nc.vector.tensor_scalar_add(bias1[:], bias[:], 1.0)
 
         acc0 = [ps_y.tile([P, HALF], F32, name="acc") for c in range(4)]
         for c0 in (0, 2):
@@ -234,9 +246,13 @@ def tile_list_xcross_none_kernel(
         quant_h(1, 1)
         for c in range(4):
             finish(acc0[c], 0, c)
+        acc1 = [ps_h.tile([P, HALF], F32, name="bank") for c in range(4)]
         for c in range(4):
-            acc = ps_h.tile([P, HALF], F32, name="bank")
-            y_wb(acc, 1, c)
-            for g in range(2):
-                y_up(acc, 1, c, g)
-            finish(acc, 1, c)
+            y_wb(acc1[c], 1, c)
+            y_up(acc1[c], 1, c, 0)
+        for c in range(4):
+            y_up(acc1[c], 1, c, 1)
+        for c in range(3):
+            finish(acc1[c], 1, c)
+        finish(acc1[3], 1, 3, 0, HALF // 2)
+        finish(acc1[3], 1, 3, HALF // 2, HALF)

@@ -19,7 +19,7 @@ MULT = mybir.AluOpType.mult
 
 P = 128
 HALF = 512
-CH = 128
+CH = 256
 
 
 def tile_list_xcross_none_kernel(
@@ -133,22 +133,21 @@ def tile_list_xcross_none_kernel(
             return dict(rhs=tp[h][:, HALF * a : HALF * (a + 1)][:, cols].bitcast(FP4X4), rhs_scale=plane[:, cols])
 
         def h_chunk(h, g, c):
-            bank = ps_h.tile([P, 4, CH], F32, name="bank")
-            cols = slice(CH * c, CH * (c + 1))
-            for t in range(4):
+            q, u = divmod(c, 2)
+            bank = ps_h.tile([P, 2, CH], F32, name="bank")
+            cols = slice(CH * q, CH * (q + 1))
+            for e in range(2):
+                t = 2 * u + e
                 for a in range(2):
                     nc.tensor.matmul_mx(
-                        out=bank[:, t, :],
+                        out=bank[:, e, :],
                         lhsT=dw[g][:, a, 64 * t : 64 * (t + 1)].bitcast(FP4X4),
                         lhsT_scale=ds[g][:, a, 32 * t : 32 * (t + 1)].bitcast(U8),
                         start=(a == 0),
                         stop=(a == 1),
                         **tab_operand(h, a, cols),
                     )
-            nc.scalar.copy(
-                hb[h][g][:, cols, :].rearrange("p (c i) t -> p c t i", i=2),
-                bank[:].rearrange("p t (c i) -> p c t i", i=2),
-            )
+            nc.scalar.copy(hb[h][g][:, cols, 2 * u : 2 * u + 2], bank[:].rearrange("p e j -> p j e"))
 
         def quant_h(h, g):
             nc.vector.quantize_mx(

@@ -16,10 +16,15 @@ FP8X4 = mybir.dt.float8_e4m3fn_x4
 FP4X4 = mybir.dt.float4_e2m1fn_x4
 ADD = mybir.AluOpType.add
 MULT = mybir.AluOpType.mult
+COPY = mybir.ActivationFunctionType.Copy
 
 P = 128
-HALF = 512
-CH = 256
+HALF = J // 2
+QUARTER = J // 4
+PER_COLUMN = 16
+PLANE_GAP = 16
+KB = 1024
+PIECES = ((0, QUARTER), (QUARTER, HALF), (HALF, J))
 
 
 def tile_list_xcross_none_kernel(
@@ -32,72 +37,77 @@ def tile_list_xcross_none_kernel(
         ps_h = ctx.enter_context(tc.psum_pool(name="ps_h", bufs=4))
         ps_y = ctx.enter_context(tc.psum_pool(name="ps_y", bufs=4))
 
-        def kt(shape, dt, name):
-            return keep.tile(shape, dt, name=name, align_bytes=64)
+        def own(shape, dtype, name):
+            return keep.tile(shape, dtype, name=name, align_bytes=64)
 
-        def st(shape, dt, name, offset):
-            return shared.tile(shape, dt, name=name, align_bytes=64, offset=offset)
+        def placed(shape, dtype, name, offset):
+            return shared.tile(shape, dtype, name=name, align_bytes=64, offset=offset)
 
-        lst = keep.tile([P, J // 16], U16, name="lst")
-        bias1 = kt([P, 4], F32, "bias1")
-        gs = kt([P, J], U8, "gs")
-        sh = kt([P, J], U8, "sh")
-        tp = [kt([P, 2 * HALF], U16, f"tp{h}") for h in range(2)]
-        dw = [kt([P, 2, 256], I32, f"dw{g}") for g in range(2)]
-        ds = [kt([P, 2, 128], I32, f"ds{g}") for g in range(2)]
-        up_bf = [kt([P, N, 4], BF16, f"up_bf{g}") for g in range(2)]
-        up_s = [kt([P, N], U8, f"up_s{g}") for g in range(2)]
-        hs = [[kt([P, HALF], U8, f"hs{h}_{g}") for g in range(2)] for h in range(2)]
+        entries = keep.tile([P, J // PER_COLUMN], U16, name="entries")
+        bias_plus_1 = own([P, 4], F32, "bias_plus_1")
+        tab_plane = [own([P, J], U8, f"tab_plane{a}") for a in range(2)]
+        tab_parted = [own([P, 2 * HALF], U16, f"tab_parted{h}") for h in range(2)]
+        dn_w = [own([P, 2, 256], I32, f"dn_w{g}") for g in range(2)]
+        dn_s = [own([P, 2, 128], I32, f"dn_s{g}") for g in range(2)]
+        up_bf = [own([P, N, 4], BF16, f"up_bf{g}") for g in range(2)]
+        up_s = [own([P, N], U8, f"up_s{g}") for g in range(2)]
+        h_s = [[own([P, HALF], U8, f"h_s{h}_{g}") for g in range(2)] for h in range(2)]
+        bias_rows = own([P, P], F32, "bias_rows")
+        ident = own([P, P], F32, "ident")
 
-        KB = 1024
-        zeros = st([P, 1056], I32, "zeros", 8 * KB - 64)
-        tw = st([P, T], U32, "tw", 0)
-        dw_raw = st([P, 2, R // 2], I32, "dw_raw", 8 * KB)
-        ts = st([P, T], U8, "ts", 21 * KB + 512)
-        ds_raw = st([P, 2, R // 4], I32, "ds_raw", 38 * KB)
-        ww = st([P, 2, N // 2], I32, "ww", 20 * KB)
-        bias = kt([P, P], F32, "bias")
-        ident = kt([P, P], F32, "ident")
-        ws = st([P, 2, N // 4], I32, "ws", 47 * KB)
-        up_raw = [st([P, 4, N], F32, "up_raw0", 12 * KB), st([P, 4, N], F32, "up_raw1", 31 * KB)]
-        xs = [st([P, T], F32, f"xs{c}", at * KB) for c, at in enumerate((23, 39, 0, 12))]
-        xg = [st([P, J], F32, "xg0", 8 * KB)] + [kt([P, J], F32, f"xg{c}") for c in range(1, 4)]
-        pieces = [(0, 256), (256, 512), (512, 1024)]
-        gw = [st([P, hi - lo], U32, f"gw{i}", at * KB) for i, ((lo, hi), at) in enumerate(zip(pieces, (47, 8, 9)))]
-        hb = [
-            [kt([P, HALF, 4], BF16, f"hb0_{g}") for g in range(2)],
-            [kt([P, HALF, 4], BF16, "hb1_0"), st([P, HALF, 4], BF16, "hb1_1", 48 * KB)],
+        zeros = placed([P, (4 * KB + 128) // 4], I32, "zeros", 8 * KB - 64)
+        tab_w = placed([P, T], U32, "tab_w", 0)
+        dn_w_raw = placed([P, 2, R // 2], I32, "dn_w_raw", 8 * KB)
+        tab_s = placed([P, T], U8, "tab_s", 21 * KB + 512)
+        dn_s_raw = placed([P, 2, R // 4], I32, "dn_s_raw", 38 * KB)
+        wb_w = placed([P, 2, N // 2], I32, "wb_w", 20 * KB)
+        wb_s = placed([P, 2, N // 4], I32, "wb_s", 47 * KB)
+        up_raw = [placed([P, 4, N], F32, f"up_raw{g}", at * KB) for g, at in enumerate((12, 31))]
+        x = [placed([P, T], F32, f"x{c}", at * KB) for c, at in enumerate((23, 39, 0, 12))]
+        picked_x = [placed([P, J], F32, "picked_x0", 8 * KB)] + [own([P, J], F32, f"picked_x{c}") for c in (1, 2, 3)]
+        picked_w = [
+            placed([P, hi - lo], U32, f"picked_w{i}", at * KB) for i, ((lo, hi), at) in enumerate(zip(PIECES, (47, 8, 9)))
         ]
-        up_c = [kt([P, N], U32, "up_c0"), st([P, N], U32, "up_c1", 41 * KB)]
-        hc = [
-            [kt([P, HALF], U32, f"hc0_{g}") for g in range(2)],
-            [st([P, HALF], U32, "hc1_0", 0), st([P, HALF], U32, "hc1_1", 12 * KB)],
+        h_bf = [
+            [own([P, HALF, 4], BF16, f"h_bf0_{g}") for g in range(2)],
+            [own([P, HALF, 4], BF16, "h_bf1_0"), placed([P, HALF, 4], BF16, "h_bf1_1", 32 * KB)],
         ]
-        res = [
-            [st([P, HALF], F32, f"o0_{c}", at * KB) for c, at in enumerate((2, 4, 48, 50))],
-            [kt([P, HALF], F32, f"o1_{c}") for c in range(4)],
+        up_c = [own([P, N], U32, "up_c0"), placed([P, N], U32, "up_c1", 6 * KB)]
+        h_c = [
+            [placed([P, HALF], U32, f"h_c0_{g}", at * KB) for g, at in enumerate((24, 26))],
+            [placed([P, HALF], U32, f"h_c1_{g}", at * KB) for g, at in enumerate((0, 12))],
+        ]
+        result = [
+            [placed([P, HALF], F32, f"result0_{c}", at * KB) for c, at in enumerate((2, 4, 32, 34))],
+            [own([P, HALF], F32, f"result1_{c}") for c in range(4)],
         ]
 
-        nc.gpsimd.memset(ts[:].bitcast(I32), 0)
-        nc.gpsimd.memset(bias[:], 0.0)
+        nc.gpsimd.memset(tab_s[:].bitcast(I32), 0)
+        nc.gpsimd.memset(bias_rows[:], 0.0)
         make_identity(nc, ident[:])
-        nc.vector.memset(zeros[:, 0:256], 0)
-        nc.vector.tensor_copy(sh[:].bitcast(I32), zeros[:, 0:256])
-        nc.vector.memset(ds_raw[:], 0)
+        nc.vector.memset(zeros[:, 0 : J // 4], 0)
+        nc.vector.tensor_copy(tab_plane[1][:].bitcast(I32), zeros[:, 0 : J // 4])
+        nc.vector.memset(dn_s_raw[:], 0)
 
-        nc.sync.dma_start(lst[:], offs)
-        ts_src = tab_scales.bitcast(I32).rearrange("a (q r) c -> r q a c", r=4)
-        for r in range(4):
-            nc.sync.dma_start(ts[:].bitcast(I32)[r:P:16, :], ts_src[r])
-        nc.sync.dma_start(tw[:].bitcast(I32), tab_words[0].rearrange("p t b -> p (t b)").bitcast(I32))
-        ds_src = dn_scales.bitcast(I32).rearrange("a q c -> q a c")
-        for q in range(4):
-            nc.sync.dma_start(ds_raw[32 * q : 32 * q + 4], ds_src[4 * q : 4 * q + 4])
-        nc.sync.dma_start(dw_raw[:], dn_words.bitcast(I32).rearrange("a p c -> p a c"))
-        nc.scalar.dma_start(bias[0:4, :], b.rearrange("(c p) -> c p", p=P))
+        nc.sync.dma_start(entries[:], offs)
+        tab_s_src = tab_scales.bitcast(I32).rearrange("a (q m) c -> m q a c", m=4)
+        for m in range(4):
+            nc.sync.dma_start(tab_s[:].bitcast(I32)[m:P:PLANE_GAP, :], tab_s_src[m])
+        nc.sync.dma_start(tab_w[:].bitcast(I32), tab_words[0].rearrange("p t b -> p (t b)").bitcast(I32))
+
+        def load_planes(planes, scales):
+            src = scales.bitcast(I32).rearrange("a q c -> q a c")
+            for q in range(4):
+                nc.sync.dma_start(planes[32 * q : 32 * q + 4], src[4 * q : 4 * q + 4])
+
+        load_planes(dn_s_raw, dn_scales)
+        nc.sync.dma_start(dn_w_raw[:], dn_words.bitcast(I32).rearrange("a p c -> p a c"))
+
+        nc.scalar.dma_start(bias_rows[0:4, :], b.rearrange("(c p) -> c p", p=P))
         turned = ps_h.tile([P, P], F32, name="bank")
-        nc.tensor.transpose(turned[:], bias[:], ident[:])
-        nc.scalar.activation(bias1[:], turned[:, 0:4], mybir.ActivationFunctionType.Copy, bias=1.0)
+        nc.tensor.transpose(turned[:], bias_rows[:], ident[:])
+        nc.scalar.activation(bias_plus_1[:], turned[:, 0:4], COPY, bias=1.0)
+
         up_src = upw.rearrange("(g u t i) n -> g t u i n", g=2, t=4, i=8)
 
         def load_up(g):
@@ -105,53 +115,59 @@ def tile_list_xcross_none_kernel(
                 nc.sync.dma_start(up_raw[g][:, t, :], up_src[g][t])
 
         def load_x(c):
-            nc.sync.dma_start(xs[c][:], x0T[P * c : P * (c + 1), :])
+            nc.sync.dma_start(x[c][:], x0T[P * c : P * (c + 1), :])
+
+        def listed(lo, hi):
+            return entries[:, lo // PER_COLUMN : hi // PER_COLUMN]
 
         def gather_scales(lo, hi):
-            nc.vector.tensor_copy(gs[:, lo:hi], ts[:].indirect(lst[:, lo // 16 : hi // 16]))
+            nc.vector.tensor_copy(tab_plane[0][:, lo:hi], tab_s[:].indirect(listed(lo, hi)))
             words = slice(lo // 4, hi // 4)
-            nc.scalar.dma_start(sh[:].bitcast(I32)[0:112, words], gs[:].bitcast(I32)[16:128, words])
+            nc.scalar.dma_start(
+                tab_plane[1][:].bitcast(I32)[0 : P - PLANE_GAP, words], tab_plane[0][:].bitcast(I32)[PLANE_GAP:P, words]
+            )
 
         def gather_words(i):
-            lo, hi = pieces[i]
-            nc.vector.tensor_copy(gw[i][:], tw[:].indirect(lst[:, lo // 16 : hi // 16]))
-            parted = tp[lo // HALF][:].rearrange("p (d j) -> p d j", d=2)[:, :, lo % HALF : lo % HALF + hi - lo]
-            nc.vector.tensor_copy(parted, gw[i][:].bitcast(U16).rearrange("p (j d) -> p d j", d=2))
+            lo, hi = PIECES[i]
+            nc.vector.tensor_copy(picked_w[i][:], tab_w[:].indirect(listed(lo, hi)))
+            parted = tab_parted[lo // HALF][:].rearrange("p (a j) -> p a j", a=2)[:, :, lo % HALF : lo % HALF + hi - lo]
+            nc.vector.tensor_copy(parted, picked_w[i][:].bitcast(U16).rearrange("p (j a) -> p a j", a=2))
 
-        def deal_dn(g):
+        def order_dn(g):
             nc.vector.tensor_copy(
-                dw[g][:].rearrange("p a (t u w) -> p a t u w", t=4, w=4),
-                dw_raw[:, :, 256 * g : 256 * (g + 1)].rearrange("p a (u t w) -> p a t u w", t=4, w=4),
+                dn_w[g][:].rearrange("p a (t u w) -> p a t u w", t=4, w=4),
+                dn_w_raw[:, :, 256 * g : 256 * (g + 1)].rearrange("p a (u t w) -> p a t u w", t=4, w=4),
             )
             nc.vector.tensor_copy(
-                ds[g][:].rearrange("p a (t u w) -> p a t u w", t=4, w=2),
-                ds_raw[:, :, 128 * g : 128 * (g + 1)].rearrange("p a (u t w) -> p a t u w", t=4, w=2),
+                dn_s[g][:].rearrange("p a (t u w) -> p a t u w", t=4, w=2),
+                dn_s_raw[:, :, 128 * g : 128 * (g + 1)].rearrange("p a (u t w) -> p a t u w", t=4, w=2),
             )
 
-        def tab_operand(h, a, cols):
-            plane = (gs, sh)[a][:, HALF * h : HALF * (h + 1)]
-            return dict(rhs=tp[h][:, HALF * a : HALF * (a + 1)][:, cols].bitcast(FP4X4), rhs_scale=plane[:, cols])
+        def table_operand(h, a, cols):
+            return dict(
+                rhs=tab_parted[h][:, HALF * a : HALF * (a + 1)][:, cols].bitcast(FP4X4),
+                rhs_scale=tab_plane[a][:, HALF * h : HALF * (h + 1)][:, cols],
+            )
 
-        def h_chunk(h, g, c):
-            q, u = divmod(c, 2)
-            bank = ps_h.tile([P, 2, CH], F32, name="bank")
-            cols = slice(CH * q, CH * (q + 1))
+        def h_bank(h, g, q, pair):
+            bank = ps_h.tile([P, 2, QUARTER], F32, name="bank")
+            cols = slice(QUARTER * q, QUARTER * (q + 1))
             for e in range(2):
-                t = 2 * u + e
+                t = 2 * pair + e
                 for a in range(2):
                     nc.tensor.matmul_mx(
                         out=bank[:, e, :],
-                        lhsT=dw[g][:, a, 64 * t : 64 * (t + 1)].bitcast(FP4X4),
-                        lhsT_scale=ds[g][:, a, 32 * t : 32 * (t + 1)].bitcast(U8),
+                        lhsT=dn_w[g][:, a, 64 * t : 64 * (t + 1)].bitcast(FP4X4),
+                        lhsT_scale=dn_s[g][:, a, 32 * t : 32 * (t + 1)].bitcast(U8),
                         start=(a == 0),
                         stop=(a == 1),
-                        **tab_operand(h, a, cols),
+                        **table_operand(h, a, cols),
                     )
-            nc.scalar.copy(hb[h][g][:, cols, 2 * u : 2 * u + 2], bank[:].rearrange("p e j -> p j e"))
+            nc.scalar.copy(h_bf[h][g][:, cols, 2 * pair : 2 * pair + 2], bank[:].rearrange("p e j -> p j e"))
 
-        def quant_h(h, g):
+        def quantise_h(h, g):
             nc.vector.quantize_mx(
-                out=hc[h][g][:].bitcast(FP8X4), scales=hs[h][g][:], in_=hb[h][g][:].rearrange("p j t -> p (j t)")
+                out=h_c[h][g][:].bitcast(FP8X4), scales=h_s[h][g][:], in_=h_bf[h][g][:].rearrange("p j t -> p (j t)")
             )
 
         def cast_up(g, copy, lo, hi):
@@ -160,98 +176,100 @@ def tile_list_xcross_none_kernel(
                 up_raw[g][:, :, lo:hi].rearrange("p t (c i) -> p c t i", i=4),
             )
 
-        def quant_up(g):
+        def quantise_up(g):
             nc.vector.quantize_mx(
                 out=up_c[g][:].bitcast(FP8X4), scales=up_s[g][:], in_=up_bf[g][:].rearrange("p n t -> p (n t)")
             )
 
-        def y_wb(acc, h, c):
+        def y_from_wb(acc, h, c):
             for a in range(2):
                 nc.tensor.matmul_mx(
                     out=acc[:],
-                    lhsT=ww[:, a, 64 * c : 64 * (c + 1)].bitcast(FP4X4),
-                    lhsT_scale=ws[:, a, 32 * c : 32 * (c + 1)].bitcast(U8),
+                    lhsT=wb_w[:, a, 64 * c : 64 * (c + 1)].bitcast(FP4X4),
+                    lhsT_scale=wb_s[:, a, 32 * c : 32 * (c + 1)].bitcast(U8),
                     start=(a == 0),
                     stop=False,
-                    **tab_operand(h, a, slice(0, HALF)),
+                    **table_operand(h, a, slice(0, HALF)),
                 )
 
-        def y_up(acc, h, c, g):
+        def y_from_up(acc, h, c, g):
             cols = slice(P * c, P * (c + 1))
             nc.tensor.matmul_mx(
                 out=acc[:],
                 lhsT=up_c[g][:, cols].bitcast(FP8X4),
                 lhsT_scale=up_s[g][:, cols],
-                rhs=hc[h][g][:].bitcast(FP8X4),
-                rhs_scale=hs[h][g][:],
+                rhs=h_c[h][g][:].bitcast(FP8X4),
+                rhs_scale=h_s[h][g][:],
                 start=False,
                 stop=(g == 1),
             )
 
         def gather_x(c):
-            nc.vector.tensor_copy(xg[c][:], xs[c][:].indirect(lst[:]))
+            nc.vector.tensor_copy(picked_x[c][:], x[c][:].indirect(entries[:]))
 
         def finish(acc, h, c, lo=0, hi=HALF):
-            o = res[h][c][:, lo:hi]
+            done = result[h][c][:, lo:hi]
             cols = slice(HALF * h + lo, HALF * h + hi)
-            nc.vector.scalar_tensor_tensor(o, acc[:, lo:hi], bias1[:, c : c + 1], xg[c][:, cols], ADD, MULT)
-            nc.sync.dma_start(out[P * c : P * (c + 1), cols], o)
+            nc.vector.scalar_tensor_tensor(done, acc[:, lo:hi], bias_plus_1[:, c : c + 1], picked_x[c][:, cols], ADD, MULT)
+            nc.sync.dma_start(out[P * c : P * (c + 1), cols], done)
 
         load_up(0)
-        gather_scales(0, 256)
-        gather_scales(256, J)
+        gather_scales(0, QUARTER)
+        gather_scales(QUARTER, J)
         gather_words(0)
-        deal_dn(0)
-        deal_dn(1)
+        order_dn(0)
+        order_dn(1)
         load_x(0)
-        nc.sync.dma_start(ww[:], wb_words.bitcast(I32).rearrange("a p c -> p a c"))
-        nc.gpsimd.memset(ws[:], 0)
-        ws_src = wb_scales.bitcast(I32).rearrange("a q c -> q a c")
-        for q in range(4):
-            nc.sync.dma_start(ws[32 * q : 32 * q + 4], ws_src[4 * q : 4 * q + 4])
-        load_up(1)
+        nc.sync.dma_start(wb_w[:], wb_words.bitcast(I32).rearrange("a p c -> p a c"))
+        nc.gpsimd.memset(wb_s[:], 0)
+        load_planes(wb_s, wb_scales)
         load_x(1)
+        load_up(1)
         gather_words(1)
         gather_words(2)
         load_x(2)
         cast_up(0, nc.vector.tensor_copy, 0, N)
         load_x(3)
-        quant_up(0)
+        quantise_up(0)
         gather_x(0)
 
         acc0 = [ps_y.tile([P, HALF], F32, name="acc") for c in range(4)]
-        for c0 in (0, 2):
+        for q in range(2):
             for g in range(2):
-                for c in (c0, c0 + 1):
-                    h_chunk(0, g, c)
-                    if c0 == 2:
-                        y_wb(acc0[2 * g + c - 2], 0, 2 * g + c - 2)
-        quant_h(0, 0)
-        quant_h(0, 1)
+                for pair in range(2):
+                    h_bank(0, g, q, pair)
+                    if q == 1:
+                        y_from_wb(acc0[2 * g + pair], 0, 2 * g + pair)
+        quantise_h(0, 0)
+        quantise_h(0, 1)
         cast_up(1, nc.scalar.copy, 0, N // 2)
         cast_up(1, nc.scalar.copy, N // 2, N)
         gather_x(1)
-        quant_up(1)
-        for c in range(4):
-            h_chunk(1, 0, c)
+
+        for q in range(2):
+            for pair in range(2):
+                h_bank(1, 0, q, pair)
         gather_x(2)
-        quant_h(1, 0)
+        quantise_up(1)
+        quantise_h(1, 0)
         for c in range(4):
             for g in range(2):
-                y_up(acc0[c], 0, c, g)
-        for c in range(4):
-            h_chunk(1, 1, c)
+                y_from_up(acc0[c], 0, c, g)
+        for q in range(2):
+            for pair in range(2):
+                h_bank(1, 1, q, pair)
         gather_x(3)
-        quant_h(1, 1)
+        quantise_h(1, 1)
         for c in range(4):
             finish(acc0[c], 0, c)
+
         acc1 = [ps_h.tile([P, HALF], F32, name="bank") for c in range(4)]
         for c in range(4):
-            y_wb(acc1[c], 1, c)
-            y_up(acc1[c], 1, c, 0)
+            y_from_wb(acc1[c], 1, c)
+            y_from_up(acc1[c], 1, c, 0)
         for c in range(4):
-            y_up(acc1[c], 1, c, 1)
+            y_from_up(acc1[c], 1, c, 1)
         for c in range(3):
             finish(acc1[c], 1, c)
-        finish(acc1[3], 1, 3, 0, HALF // 2)
-        finish(acc1[3], 1, 3, HALF // 2, HALF)
+        finish(acc1[3], 1, 3, 0, QUARTER)
+        finish(acc1[3], 1, 3, QUARTER, HALF)

@@ -1,7 +1,6 @@
 from contextlib import ExitStack
 
 import concourse.mybir as mybir
-from concourse.masks import make_identity
 
 K, R, N, T, J = 1024, 1024, 512, 2048, 1024
 FLOPS = 2 * J * (K * R + K * N + R * N)
@@ -16,7 +15,7 @@ FP8X4 = mybir.dt.float8_e4m3fn_x4
 FP4X4 = mybir.dt.float4_e2m1fn_x4
 ADD = mybir.AluOpType.add
 MULT = mybir.AluOpType.mult
-COPY = mybir.ActivationFunctionType.Copy
+IDENTITY = mybir.ActivationFunctionType.Identity
 
 P = 128
 HALF = J // 2
@@ -24,6 +23,7 @@ QUARTER = J // 4
 PER_COLUMN = 16
 PLANE_GAP = 16
 KB = 1024
+AHEAD = ((0, 0), (1, 0), (1, 1), (1, 2))
 PIECES = ((0, QUARTER), (QUARTER, HALF), (HALF, J))
 
 
@@ -45,49 +45,42 @@ def tile_list_xcross_none_kernel(
 
         entries = keep.tile([P, J // PER_COLUMN], U16, name="entries")
         bias_plus_1 = own([P, 4], F32, "bias_plus_1")
+        tab_s = own([P, T], U8, "tab_s")
         tab_plane = [own([P, J], U8, f"tab_plane{a}") for a in range(2)]
         tab_parted = [own([P, 2 * HALF], U16, f"tab_parted{h}") for h in range(2)]
         dn_w = [own([P, 2, 256], I32, f"dn_w{g}") for g in range(2)]
-        dn_s = [own([P, 2, 128], I32, f"dn_s{g}") for g in range(2)]
+        dn_s = own([P, 2, 2, 128], I32, "dn_s")
+        wb_s = own([P, 2, N // 4], I32, "wb_s")
         up_bf = [own([P, N, 4], BF16, f"up_bf{g}") for g in range(2)]
         up_s = [own([P, N], U8, f"up_s{g}") for g in range(2)]
+        up_c = [own([P, N], U32, f"up_c{g}") for g in range(2)]
+        h_bf = [[own([P, HALF, 4], BF16, f"h_bf{h}_{g}") for g in range(2)] for h in range(2)]
         h_s = [[own([P, HALF], U8, f"h_s{h}_{g}") for g in range(2)] for h in range(2)]
-        bias_rows = own([P, P], F32, "bias_rows")
-        ident = own([P, P], F32, "ident")
+        h_c = [[own([P, HALF], U32, f"h_c{h}_{g}") for g in range(2)] for h in range(2)]
+        picked_x = {hc: own([P, HALF], F32, "picked_x%d_%d" % hc) for hc in AHEAD}
+        y_sb = {(h, c): own([P, HALF], F32, f"y_sb{h}_{c}") for h in range(2) for c in range(4) if (h, c) not in AHEAD}
+        result = [[own([P, HALF], F32, f"result{h}_{c}") for c in range(4)] for h in range(2)]
 
-        zeros = placed([P, (4 * KB + 128) // 4], I32, "zeros", 8 * KB - 64)
+        zeros = placed([P, 20 * KB // 4], I32, "zeros", 0)
         tab_w = placed([P, T], U32, "tab_w", 0)
         dn_w_raw = placed([P, 2, R // 2], I32, "dn_w_raw", 8 * KB)
-        tab_s = placed([P, T], U8, "tab_s", 21 * KB + 512)
-        dn_s_raw = placed([P, 2, R // 4], I32, "dn_s_raw", 38 * KB)
-        wb_w = placed([P, 2, N // 2], I32, "wb_w", 20 * KB)
-        wb_s = placed([P, 2, N // 4], I32, "wb_s", 47 * KB)
-        up_raw = [placed([P, 4, N], F32, f"up_raw{g}", at * KB) for g, at in enumerate((12, 31))]
-        x = [placed([P, T], F32, f"x{c}", at * KB) for c, at in enumerate((23, 39, 0, 12))]
-        picked_x = [placed([P, J], F32, "picked_x0", 8 * KB)] + [own([P, J], F32, f"picked_x{c}") for c in (1, 2, 3)]
+        dn_s_raw = placed([P, 2, R // 4], I32, "dn_s_raw", 20 * KB)
+        first_picked = placed([P, (42 * KB + 64) // 4], U32, "picked_w0", 24 * KB)
         picked_w = [
-            placed([P, hi - lo], U32, f"picked_w{i}", at * KB) for i, ((lo, hi), at) in enumerate(zip(PIECES, (47, 8, 9)))
+            first_picked[:, 0:QUARTER],
+            placed([P, QUARTER], U32, "picked_w1", 20 * KB)[:],
+            placed([P, HALF], U32, "picked_w2", 21 * KB)[:],
         ]
-        h_bf = [
-            [own([P, HALF, 4], BF16, f"h_bf0_{g}") for g in range(2)],
-            [own([P, HALF, 4], BF16, "h_bf1_0"), placed([P, HALF, 4], BF16, "h_bf1_1", 32 * KB)],
-        ]
-        up_c = [own([P, N], U32, "up_c0"), placed([P, N], U32, "up_c1", 6 * KB)]
-        h_c = [
-            [placed([P, HALF], U32, f"h_c0_{g}", at * KB) for g, at in enumerate((24, 26))],
-            [placed([P, HALF], U32, f"h_c1_{g}", at * KB) for g, at in enumerate((0, 12))],
-        ]
-        result = [
-            [placed([P, HALF], F32, f"result0_{c}", at * KB) for c, at in enumerate((2, 4, 32, 34))],
-            [own([P, HALF], F32, f"result1_{c}") for c in range(4)],
-        ]
+        wb_w = placed([P, 2, N // 2], I32, "wb_w", 24 * KB)
+        up_raw = [placed([P, 4, N], F32, f"up_raw{g}", at * KB) for g, at in enumerate((26, 42))]
+        x = [placed([P, T], F32, f"x{c}", at * KB) for c, at in enumerate((12, 34, 50, 58))]
+        bias = own([P, 4], F32, "bias")
 
         nc.gpsimd.memset(tab_s[:].bitcast(I32), 0)
-        nc.gpsimd.memset(bias_rows[:], 0.0)
-        make_identity(nc, ident[:])
-        nc.vector.memset(zeros[:, 0 : J // 4], 0)
-        nc.vector.tensor_copy(tab_plane[1][:].bitcast(I32), zeros[:, 0 : J // 4])
-        nc.vector.memset(dn_s_raw[:], 0)
+        nc.vector.memset(zeros[:, 0 : R // 2], 0)
+        nc.vector.tensor_copy(dn_s_raw[:].rearrange("p a c -> p (a c)"), zeros[:, 0 : R // 2])
+        nc.vector.memset(tab_plane[1][:].bitcast(I32), 0)
+        nc.vector.memset(wb_s[:], 0)
 
         nc.sync.dma_start(entries[:], offs)
         tab_s_src = tab_scales.bitcast(I32).rearrange("a (q m) c -> m q a c", m=4)
@@ -95,18 +88,14 @@ def tile_list_xcross_none_kernel(
             nc.sync.dma_start(tab_s[:].bitcast(I32)[m:P:PLANE_GAP, :], tab_s_src[m])
         nc.sync.dma_start(tab_w[:].bitcast(I32), tab_words[0].rearrange("p t b -> p (t b)").bitcast(I32))
 
-        def load_planes(planes, scales):
+        def load_planes(queue, planes, scales):
             src = scales.bitcast(I32).rearrange("a q c -> q a c")
             for q in range(4):
-                nc.sync.dma_start(planes[32 * q : 32 * q + 4], src[4 * q : 4 * q + 4])
+                queue.dma_start(planes[32 * q : 32 * q + 4], src[4 * q : 4 * q + 4])
 
-        load_planes(dn_s_raw, dn_scales)
         nc.sync.dma_start(dn_w_raw[:], dn_words.bitcast(I32).rearrange("a p c -> p a c"))
-
-        nc.scalar.dma_start(bias_rows[0:4, :], b.rearrange("(c p) -> c p", p=P))
-        turned = ps_h.tile([P, P], F32, name="bank")
-        nc.tensor.transpose(turned[:], bias_rows[:], ident[:])
-        nc.scalar.activation(bias_plus_1[:], turned[:, 0:4], COPY, bias=1.0)
+        load_planes(nc.sync, dn_s_raw, dn_scales)
+        load_planes(nc.gpsimd, wb_s, wb_scales)
 
         up_src = upw.rearrange("(g u t i) n -> g t u i n", g=2, t=4, i=8)
 
@@ -129,18 +118,20 @@ def tile_list_xcross_none_kernel(
 
         def gather_words(i):
             lo, hi = PIECES[i]
-            nc.vector.tensor_copy(picked_w[i][:], tab_w[:].indirect(listed(lo, hi)))
+            nc.vector.tensor_copy(picked_w[i], tab_w[:].indirect(listed(lo, hi)))
             parted = tab_parted[lo // HALF][:].rearrange("p (a j) -> p a j", a=2)[:, :, lo % HALF : lo % HALF + hi - lo]
-            nc.vector.tensor_copy(parted, picked_w[i][:].bitcast(U16).rearrange("p (j a) -> p a j", a=2))
+            nc.vector.tensor_copy(parted, picked_w[i].bitcast(U16).rearrange("p (j a) -> p a j", a=2))
 
         def order_dn(g):
             nc.vector.tensor_copy(
                 dn_w[g][:].rearrange("p a (t u w) -> p a t u w", t=4, w=4),
                 dn_w_raw[:, :, 256 * g : 256 * (g + 1)].rearrange("p a (u t w) -> p a t u w", t=4, w=4),
             )
+
+        def order_dn_scales():
             nc.vector.tensor_copy(
-                dn_s[g][:].rearrange("p a (t u w) -> p a t u w", t=4, w=2),
-                dn_s_raw[:, :, 128 * g : 128 * (g + 1)].rearrange("p a (u t w) -> p a t u w", t=4, w=2),
+                dn_s[:].rearrange("p a g (t u w) -> p (a g) t u w", t=4, w=2),
+                dn_s_raw[:].rearrange("p a (g u t w) -> p (a g) t u w", g=2, t=4, w=2),
             )
 
         def table_operand(h, a, cols):
@@ -158,7 +149,7 @@ def tile_list_xcross_none_kernel(
                     nc.tensor.matmul_mx(
                         out=bank[:, e, :],
                         lhsT=dn_w[g][:, a, 64 * t : 64 * (t + 1)].bitcast(FP4X4),
-                        lhsT_scale=dn_s[g][:, a, 32 * t : 32 * (t + 1)].bitcast(U8),
+                        lhsT_scale=dn_s[:, a, g, 32 * t : 32 * (t + 1)].bitcast(U8),
                         start=(a == 0),
                         stop=(a == 1),
                         **table_operand(h, a, cols),
@@ -204,34 +195,44 @@ def tile_list_xcross_none_kernel(
                 stop=(g == 1),
             )
 
-        def gather_x(c):
-            nc.vector.tensor_copy(picked_x[c][:], x[c][:].indirect(entries[:]))
+        def gather_x(h, c):
+            nc.vector.tensor_copy(picked_x[h, c][:], x[c][:].indirect(listed(HALF * h, HALF * (h + 1))))
+
+        def empty_y(acc, h, c):
+            nc.scalar.activation(y_sb[h, c][:], acc[:], IDENTITY, bias=bias_plus_1[:, c : c + 1])
 
         def finish(acc, h, c, lo=0, hi=HALF):
             done = result[h][c][:, lo:hi]
             cols = slice(HALF * h + lo, HALF * h + hi)
-            nc.vector.scalar_tensor_tensor(done, acc[:, lo:hi], bias_plus_1[:, c : c + 1], picked_x[c][:, cols], ADD, MULT)
+            if (h, c) in AHEAD:
+                nc.vector.scalar_tensor_tensor(
+                    done, acc[:, lo:hi], bias_plus_1[:, c : c + 1], picked_x[h, c][:, lo:hi], ADD, MULT
+                )
+            else:
+                nc.vector.tensor_tensor(done, x[c][:].indirect(listed(cols.start, cols.stop)), y_sb[h, c][:, lo:hi], MULT)
             nc.sync.dma_start(out[P * c : P * (c + 1), cols], done)
 
-        load_up(0)
+        with nc.allow_non_contiguous_dma(reason="one bias value a partition and block of rows"):
+            nc.scalar.dma_start(bias[:], b.rearrange("(c p) -> p c", p=P))
+        nc.scalar.activation(bias_plus_1[:], bias[:], IDENTITY, bias=1.0)
+        load_x(0)
         gather_scales(0, QUARTER)
         gather_scales(QUARTER, J)
         gather_words(0)
         order_dn(0)
         order_dn(1)
-        load_x(0)
+        order_dn_scales()
         nc.sync.dma_start(wb_w[:], wb_words.bitcast(I32).rearrange("a p c -> p a c"))
-        nc.gpsimd.memset(wb_s[:], 0)
-        load_planes(wb_s, wb_scales)
-        load_x(1)
+        load_up(0)
         load_up(1)
+        load_x(1)
+        load_x(2)
+        load_x(3)
         gather_words(1)
         gather_words(2)
-        load_x(2)
+        gather_x(0, 0)
+        gather_x(1, 0)
         cast_up(0, nc.vector.tensor_copy, 0, N)
-        load_x(3)
-        quantise_up(0)
-        gather_x(0)
 
         acc0 = [ps_y.tile([P, HALF], F32, name="acc") for c in range(4)]
         for q in range(2):
@@ -241,35 +242,39 @@ def tile_list_xcross_none_kernel(
                     if q == 1:
                         y_from_wb(acc0[2 * g + pair], 0, 2 * g + pair)
         quantise_h(0, 0)
+        quantise_up(0)
+        cast_up(1, nc.vector.tensor_copy, 0, N)
         quantise_h(0, 1)
-        cast_up(1, nc.scalar.copy, 0, N // 2)
-        cast_up(1, nc.scalar.copy, N // 2, N)
-        gather_x(1)
+        quantise_up(1)
+        gather_x(1, 1)
 
         for q in range(2):
             for pair in range(2):
                 h_bank(1, 0, q, pair)
-        gather_x(2)
-        quantise_up(1)
-        quantise_h(1, 0)
+            for c in range(4):
+                y_from_up(acc0[c], 0, c, q)
+        finish(acc0[0], 0, 0)
+        gather_x(1, 2)
         for c in range(4):
-            for g in range(2):
-                y_from_up(acc0[c], 0, c, g)
-        for q in range(2):
-            for pair in range(2):
-                h_bank(1, 1, q, pair)
-        gather_x(3)
+            h_bank(1, 1, c // 2, c % 2)
+            if c == 0:
+                quantise_h(1, 0)
+            if c < 3:
+                empty_y(acc0[c + 1], 0, c + 1)
+        finish(acc0[1], 0, 1)
+        finish(acc0[2], 0, 2)
         quantise_h(1, 1)
-        for c in range(4):
-            finish(acc0[c], 0, c)
+        finish(acc0[3], 0, 3)
 
-        acc1 = [ps_h.tile([P, HALF], F32, name="bank") for c in range(4)]
+        acc1 = [ps_y.tile([P, HALF], F32, name="acc") for c in range(4)]
         for c in range(4):
             y_from_wb(acc1[c], 1, c)
             y_from_up(acc1[c], 1, c, 0)
-        for c in range(4):
+        for c in (3, 0, 1, 2):
             y_from_up(acc1[c], 1, c, 1)
-        for c in range(3):
-            finish(acc1[c], 1, c)
-        finish(acc1[3], 1, 3, 0, QUARTER)
-        finish(acc1[3], 1, 3, QUARTER, HALF)
+        empty_y(acc1[3], 1, 3)
+        finish(acc1[0], 1, 0)
+        finish(acc1[3], 1, 3)
+        finish(acc1[1], 1, 1)
+        finish(acc1[2], 1, 2, 0, QUARTER)
+        finish(acc1[2], 1, 2, QUARTER, HALF)

@@ -1,6 +1,7 @@
 from contextlib import ExitStack
 
 import concourse.mybir as mybir
+from concourse.masks import make_identity
 
 K, R, N, T, J = 1024, 1024, 512, 2048, 1024
 FLOPS = 2 * J * (K * R + K * N + R * N)
@@ -24,7 +25,7 @@ PER_COLUMN = 16
 PLANE_GAP = 16
 KB = 1024
 AHEAD = ((0, 0), (1, 0), (1, 1), (1, 2))
-PIECES = ((0, QUARTER), (QUARTER, HALF), (HALF, J))
+PIECES = ((0, QUARTER), (QUARTER, J))
 
 
 def tile_list_xcross_none_kernel(
@@ -47,7 +48,7 @@ def tile_list_xcross_none_kernel(
         bias_plus_1 = own([P, 4], F32, "bias_plus_1")
         tab_s = own([P, T], U8, "tab_s")
         tab_plane = [own([P, J], U8, f"tab_plane{a}") for a in range(2)]
-        tab_parted = [own([P, 2 * HALF], U16, f"tab_parted{h}") for h in range(2)]
+        tab_parted = own([P, 2 * J], U16, "tab_parted")
         dn_w = [own([P, 2, 256], I32, f"dn_w{g}") for g in range(2)]
         dn_s = own([P, 2, 2, 128], I32, "dn_s")
         wb_s = own([P, 2, N // 4], I32, "wb_s")
@@ -57,30 +58,35 @@ def tile_list_xcross_none_kernel(
         h_bf = [[own([P, HALF, 4], BF16, f"h_bf{h}_{g}") for g in range(2)] for h in range(2)]
         h_s = [[own([P, HALF], U8, f"h_s{h}_{g}") for g in range(2)] for h in range(2)]
         h_c = [[own([P, HALF], U32, f"h_c{h}_{g}") for g in range(2)] for h in range(2)]
-        picked_x = {hc: own([P, HALF], F32, "picked_x%d_%d" % hc) for hc in AHEAD}
+        picked_x0 = own([P, J], F32, "picked_x0")
+        picked_x = {(h, 0): picked_x0[:, HALF * h : HALF * (h + 1)] for h in range(2)}
+        for c in (1, 2):
+            picked_x[1, c] = own([P, HALF], F32, f"picked_x{c}")[:]
         y_sb = {(h, c): own([P, HALF], F32, f"y_sb{h}_{c}") for h in range(2) for c in range(4) if (h, c) not in AHEAD}
         result = [[own([P, HALF], F32, f"result{h}_{c}") for c in range(4)] for h in range(2)]
 
-        zeros = placed([P, 20 * KB // 4], I32, "zeros", 0)
+        zeros = placed([P, (20 * KB + 512) // 4], I32, "zeros", 0)
         tab_w = placed([P, T], U32, "tab_w", 0)
         dn_w_raw = placed([P, 2, R // 2], I32, "dn_w_raw", 8 * KB)
-        dn_s_raw = placed([P, 2, R // 4], I32, "dn_s_raw", 20 * KB)
+        dn_s_raw = own([P, 2, R // 4], I32, "dn_s_raw")
+        ident = placed([P, P], F32, "ident", 20 * KB)
         first_picked = placed([P, (42 * KB + 64) // 4], U32, "picked_w0", 24 * KB)
         picked_w = [
             first_picked[:, 0:QUARTER],
-            placed([P, QUARTER], U32, "picked_w1", 20 * KB)[:],
-            placed([P, HALF], U32, "picked_w2", 21 * KB)[:],
+            placed([P, J - QUARTER], U32, "picked_w1", 8 * KB)[:],
         ]
         wb_w = placed([P, 2, N // 2], I32, "wb_w", 24 * KB)
         up_raw = [placed([P, 4, N], F32, f"up_raw{g}", at * KB) for g, at in enumerate((26, 42))]
         x = [placed([P, T], F32, f"x{c}", at * KB) for c, at in enumerate((12, 34, 50, 58))]
-        bias = own([P, 4], F32, "bias")
+        bias_rows = own([P, P], F32, "bias_rows")
 
         nc.gpsimd.memset(tab_s[:].bitcast(I32), 0)
+        nc.gpsimd.memset(bias_rows[:], 0.0)
         nc.vector.memset(zeros[:, 0 : R // 2], 0)
         nc.vector.tensor_copy(dn_s_raw[:].rearrange("p a c -> p (a c)"), zeros[:, 0 : R // 2])
         nc.vector.memset(tab_plane[1][:].bitcast(I32), 0)
         nc.vector.memset(wb_s[:], 0)
+        make_identity(nc, ident[:])
 
         nc.sync.dma_start(entries[:], offs)
         tab_s_src = tab_scales.bitcast(I32).rearrange("a (q m) c -> m q a c", m=4)
@@ -89,12 +95,12 @@ def tile_list_xcross_none_kernel(
         nc.sync.dma_start(tab_w[:].bitcast(I32), tab_words[0].rearrange("p t b -> p (t b)").bitcast(I32))
 
         def load_planes(queue, planes, scales):
-            src = scales.bitcast(I32).rearrange("a q c -> q a c")
-            for q in range(4):
-                queue.dma_start(planes[32 * q : 32 * q + 4], src[4 * q : 4 * q + 4])
+            src = scales.bitcast(I32).rearrange("a (q m) c -> m q a c", m=4)
+            for m in range(4):
+                queue.dma_start(planes[m:P:32], src[m])
 
-        nc.sync.dma_start(dn_w_raw[:], dn_words.bitcast(I32).rearrange("a p c -> p a c"))
         load_planes(nc.sync, dn_s_raw, dn_scales)
+        nc.sync.dma_start(dn_w_raw[:], dn_words.bitcast(I32).rearrange("a p c -> p a c"))
         load_planes(nc.gpsimd, wb_s, wb_scales)
 
         up_src = upw.rearrange("(g u t i) n -> g t u i n", g=2, t=4, i=8)
@@ -119,7 +125,7 @@ def tile_list_xcross_none_kernel(
         def gather_words(i):
             lo, hi = PIECES[i]
             nc.vector.tensor_copy(picked_w[i], tab_w[:].indirect(listed(lo, hi)))
-            parted = tab_parted[lo // HALF][:].rearrange("p (a j) -> p a j", a=2)[:, :, lo % HALF : lo % HALF + hi - lo]
+            parted = tab_parted[:].rearrange("p (a j) -> p a j", a=2)[:, :, lo:hi]
             nc.vector.tensor_copy(parted, picked_w[i].bitcast(U16).rearrange("p (j a) -> p a j", a=2))
 
         def order_dn(g):
@@ -136,7 +142,7 @@ def tile_list_xcross_none_kernel(
 
         def table_operand(h, a, cols):
             return dict(
-                rhs=tab_parted[h][:, HALF * a : HALF * (a + 1)][:, cols].bitcast(FP4X4),
+                rhs=tab_parted[:, J * a + HALF * h : J * a + HALF * (h + 1)][:, cols].bitcast(FP4X4),
                 rhs_scale=tab_plane[a][:, HALF * h : HALF * (h + 1)][:, cols],
             )
 
@@ -196,7 +202,7 @@ def tile_list_xcross_none_kernel(
             )
 
         def gather_x(h, c):
-            nc.vector.tensor_copy(picked_x[h, c][:], x[c][:].indirect(listed(HALF * h, HALF * (h + 1))))
+            nc.vector.tensor_copy(picked_x[h, c], x[c][:].indirect(listed(HALF * h, HALF * (h + 1))))
 
         def empty_y(acc, h, c):
             nc.scalar.activation(y_sb[h, c][:], acc[:], IDENTITY, bias=bias_plus_1[:, c : c + 1])
@@ -212,16 +218,17 @@ def tile_list_xcross_none_kernel(
                 nc.vector.tensor_tensor(done, x[c][:].indirect(listed(cols.start, cols.stop)), y_sb[h, c][:, lo:hi], MULT)
             nc.sync.dma_start(out[P * c : P * (c + 1), cols], done)
 
-        with nc.allow_non_contiguous_dma(reason="one bias value a partition and block of rows"):
-            nc.scalar.dma_start(bias[:], b.rearrange("(c p) -> p c", p=P))
-        nc.scalar.activation(bias_plus_1[:], bias[:], IDENTITY, bias=1.0)
+        nc.scalar.dma_start(bias_rows[0:4, :], b.rearrange("(c p) -> c p", p=P))
+        turned = ps_h.tile([P, P], F32, name="bank")
+        nc.tensor.transpose(turned[:], bias_rows[:], ident[:])
+        nc.scalar.activation(bias_plus_1[:], turned[:, 0:4], IDENTITY, bias=1.0)
         load_x(0)
         gather_scales(0, QUARTER)
         gather_scales(QUARTER, J)
         gather_words(0)
+        order_dn_scales()
         order_dn(0)
         order_dn(1)
-        order_dn_scales()
         nc.sync.dma_start(wb_w[:], wb_words.bitcast(I32).rearrange("a p c -> p a c"))
         load_up(0)
         load_up(1)
@@ -229,9 +236,7 @@ def tile_list_xcross_none_kernel(
         load_x(2)
         load_x(3)
         gather_words(1)
-        gather_words(2)
-        gather_x(0, 0)
-        gather_x(1, 0)
+        nc.vector.tensor_copy(picked_x0[:], x[0][:].indirect(entries[:]))
         cast_up(0, nc.vector.tensor_copy, 0, N)
 
         acc0 = [ps_y.tile([P, HALF], F32, name="acc") for c in range(4)]

@@ -24,8 +24,8 @@ QUARTER = J // 4
 PER_COLUMN = 16
 PLANE_GAP = 16
 KB = 1024
-AHEAD = ((0, 0), (1, 0), (1, 1), (1, 2))
-PIECES = ((0, QUARTER), (QUARTER, J))
+FUSED = ((0, 1), (0, 2), (0, 3), (1, 3))
+PIECES = ((0, QUARTER), (QUARTER, HALF), (HALF, J))
 
 
 def tile_list_xcross_none_kernel(
@@ -45,43 +45,50 @@ def tile_list_xcross_none_kernel(
             return shared.tile(shape, dtype, name=name, align_bytes=64, offset=offset)
 
         entries = keep.tile([P, J // PER_COLUMN], U16, name="entries")
+        bias_rows = own([P, P], F32, "bias_rows")
         bias_plus_1 = own([P, 4], F32, "bias_plus_1")
         tab_s = own([P, T], U8, "tab_s")
         tab_plane = [own([P, J], U8, f"tab_plane{a}") for a in range(2)]
-        tab_parted = own([P, 2 * J], U16, "tab_parted")
         dn_w = [own([P, 2, 256], I32, f"dn_w{g}") for g in range(2)]
         dn_s = own([P, 2, 2, 128], I32, "dn_s")
         wb_s = own([P, 2, N // 4], I32, "wb_s")
         up_bf = [own([P, N, 4], BF16, f"up_bf{g}") for g in range(2)]
         up_s = [own([P, N], U8, f"up_s{g}") for g in range(2)]
-        up_c = [own([P, N], U32, f"up_c{g}") for g in range(2)]
-        h_bf = [[own([P, HALF, 4], BF16, f"h_bf{h}_{g}") for g in range(2)] for h in range(2)]
         h_s = [[own([P, HALF], U8, f"h_s{h}_{g}") for g in range(2)] for h in range(2)]
-        h_c = [[own([P, HALF], U32, f"h_c{h}_{g}") for g in range(2)] for h in range(2)]
         picked_x0 = own([P, J], F32, "picked_x0")
         picked_x = {(h, 0): picked_x0[:, HALF * h : HALF * (h + 1)] for h in range(2)}
         for c in (1, 2):
             picked_x[1, c] = own([P, HALF], F32, f"picked_x{c}")[:]
-        y_sb = {(h, c): own([P, HALF], F32, f"y_sb{h}_{c}") for h in range(2) for c in range(4) if (h, c) not in AHEAD}
+        y_sb = {(h, c): own([P, HALF], F32, f"y_sb{h}_{c}") for h, c in FUSED}
         result = [[own([P, HALF], F32, f"result{h}_{c}") for c in range(4)] for h in range(2)]
 
-        zeros = placed([P, (20 * KB + 512) // 4], I32, "zeros", 0)
+        zeros = placed([P, (20 * KB + 4 * P) // 4], I32, "zeros", 0)
         tab_w = placed([P, T], U32, "tab_w", 0)
         dn_w_raw = placed([P, 2, R // 2], I32, "dn_w_raw", 8 * KB)
-        dn_s_raw = own([P, 2, R // 4], I32, "dn_s_raw")
         ident = placed([P, P], F32, "ident", 20 * KB)
-        first_picked = placed([P, (42 * KB + 64) // 4], U32, "picked_w0", 24 * KB)
+        first_picked = placed([P, 42 * KB // 4], U32, "first_picked", 24 * KB)
         picked_w = [
             first_picked[:, 0:QUARTER],
-            placed([P, J - QUARTER], U32, "picked_w1", 8 * KB)[:],
+            placed([P, QUARTER], U32, "picked_w1", 8 * KB)[:],
+            placed([P, HALF], U32, "picked_w2", 9 * KB)[:],
         ]
         wb_w = placed([P, 2, N // 2], I32, "wb_w", 24 * KB)
         up_raw = [placed([P, 4, N], F32, f"up_raw{g}", at * KB) for g, at in enumerate((26, 42))]
         x = [placed([P, T], F32, f"x{c}", at * KB) for c, at in enumerate((12, 34, 50, 58))]
-        bias_rows = own([P, P], F32, "bias_rows")
+        dn_s_raw = placed([P, 2, R // 4], I32, "dn_s_raw", 68 * KB)
+        tab_parted = placed([P, 2 * J], U16, "tab_parted", 68 * KB)
+        h_bf = [
+            [placed([P, HALF, 4], BF16, f"h_bf0_{g}", (72 + 4 * g) * KB) for g in range(2)],
+            [own([P, HALF, 4], BF16, f"h_bf1_{g}") for g in range(2)],
+        ]
+        up_c = [placed([P, N], U32, f"up_c{g}", (72 + 4 * g) * KB) for g in range(2)]
+        h_c = [
+            [placed([P, HALF], U32, f"h_c0_{g}", at * KB) for g, at in enumerate((26, 42))],
+            [own([P, HALF], U32, f"h_c1_{g}") for g in range(2)],
+        ]
 
-        nc.gpsimd.memset(tab_s[:].bitcast(I32), 0)
         nc.gpsimd.memset(bias_rows[:], 0.0)
+        nc.gpsimd.memset(tab_s[:].bitcast(I32), 0)
         nc.vector.memset(zeros[:, 0 : R // 2], 0)
         nc.vector.tensor_copy(dn_s_raw[:].rearrange("p a c -> p (a c)"), zeros[:, 0 : R // 2])
         nc.vector.memset(tab_plane[1][:].bitcast(I32), 0)
@@ -125,6 +132,9 @@ def tile_list_xcross_none_kernel(
         def gather_words(i):
             lo, hi = PIECES[i]
             nc.vector.tensor_copy(picked_w[i], tab_w[:].indirect(listed(lo, hi)))
+
+        def part_words(i):
+            lo, hi = PIECES[i]
             parted = tab_parted[:].rearrange("p (a j) -> p a j", a=2)[:, :, lo:hi]
             nc.vector.tensor_copy(parted, picked_w[i].bitcast(U16).rearrange("p (j a) -> p a j", a=2))
 
@@ -167,10 +177,9 @@ def tile_list_xcross_none_kernel(
                 out=h_c[h][g][:].bitcast(FP8X4), scales=h_s[h][g][:], in_=h_bf[h][g][:].rearrange("p j t -> p (j t)")
             )
 
-        def cast_up(g, copy, lo, hi):
-            copy(
-                up_bf[g][:, lo:hi, :].rearrange("p (c i) t -> p c t i", i=4),
-                up_raw[g][:, :, lo:hi].rearrange("p t (c i) -> p c t i", i=4),
+        def cast_up(g):
+            nc.vector.tensor_copy(
+                up_bf[g][:].rearrange("p (c i) t -> p c t i", i=4), up_raw[g][:].rearrange("p t (c i) -> p c t i", i=4)
             )
 
         def quantise_up(g):
@@ -210,34 +219,38 @@ def tile_list_xcross_none_kernel(
         def finish(acc, h, c, lo=0, hi=HALF):
             done = result[h][c][:, lo:hi]
             cols = slice(HALF * h + lo, HALF * h + hi)
-            if (h, c) in AHEAD:
+            if (h, c) in FUSED:
+                nc.vector.tensor_tensor(done, x[c][:].indirect(listed(cols.start, cols.stop)), y_sb[h, c][:, lo:hi], MULT)
+            else:
                 nc.vector.scalar_tensor_tensor(
                     done, acc[:, lo:hi], bias_plus_1[:, c : c + 1], picked_x[h, c][:, lo:hi], ADD, MULT
                 )
-            else:
-                nc.vector.tensor_tensor(done, x[c][:].indirect(listed(cols.start, cols.stop)), y_sb[h, c][:, lo:hi], MULT)
             nc.sync.dma_start(out[P * c : P * (c + 1), cols], done)
 
         nc.scalar.dma_start(bias_rows[0:4, :], b.rearrange("(c p) -> c p", p=P))
         turned = ps_h.tile([P, P], F32, name="bank")
         nc.tensor.transpose(turned[:], bias_rows[:], ident[:])
         nc.scalar.activation(bias_plus_1[:], turned[:, 0:4], IDENTITY, bias=1.0)
+
         load_x(0)
         gather_scales(0, QUARTER)
         gather_scales(QUARTER, J)
-        gather_words(0)
         order_dn_scales()
+        gather_words(0)
+        part_words(0)
         order_dn(0)
         order_dn(1)
         nc.sync.dma_start(wb_w[:], wb_words.bitcast(I32).rearrange("a p c -> p a c"))
         load_up(0)
         load_up(1)
-        load_x(1)
-        load_x(2)
-        load_x(3)
+        for c in range(1, 4):
+            load_x(c)
         gather_words(1)
+        gather_words(2)
+        part_words(1)
+        part_words(2)
         nc.vector.tensor_copy(picked_x0[:], x[0][:].indirect(entries[:]))
-        cast_up(0, nc.vector.tensor_copy, 0, N)
+        cast_up(0)
 
         acc0 = [ps_y.tile([P, HALF], F32, name="acc") for c in range(4)]
         for q in range(2):
@@ -248,7 +261,7 @@ def tile_list_xcross_none_kernel(
                         y_from_wb(acc0[2 * g + pair], 0, 2 * g + pair)
         quantise_h(0, 0)
         quantise_up(0)
-        cast_up(1, nc.vector.tensor_copy, 0, N)
+        cast_up(1)
         quantise_h(0, 1)
         quantise_up(1)
         gather_x(1, 1)
@@ -260,12 +273,11 @@ def tile_list_xcross_none_kernel(
                 y_from_up(acc0[c], 0, c, q)
         finish(acc0[0], 0, 0)
         gather_x(1, 2)
-        for c in range(4):
+        h_bank(1, 1, 0, 0)
+        quantise_h(1, 0)
+        for c in range(1, 4):
+            empty_y(acc0[c], 0, c)
             h_bank(1, 1, c // 2, c % 2)
-            if c == 0:
-                quantise_h(1, 0)
-            if c < 3:
-                empty_y(acc0[c + 1], 0, c + 1)
         finish(acc0[1], 0, 1)
         finish(acc0[2], 0, 2)
         quantise_h(1, 1)

@@ -51,9 +51,14 @@ def tile_list_xcross_none_kernel(
         tab_plane = [own([P, J], U8, f"tab_plane{a}") for a in range(2)]
         dn_w = [own([P, 2, 256], I32, f"dn_w{g}") for g in range(2)]
         dn_s = own([P, 2, 2, 128], I32, "dn_s")
+        dn_s_raw = own([P, 2, R // 4], I32, "dn_s_raw")
+        tab_parted = own([P, 2 * J], U16, "tab_parted")
         wb_s = own([P, 2, N // 4], I32, "wb_s")
         up_bf = [own([P, N, 4], BF16, f"up_bf{g}") for g in range(2)]
         up_s = [own([P, N], U8, f"up_s{g}") for g in range(2)]
+        up_c = [own([P, N], U32, f"up_c{g}") for g in range(2)]
+        h_bf = [[own([P, HALF, 4], BF16, f"h_bf{h}_{g}") for g in range(2)] for h in range(2)]
+        h_c = [[own([P, HALF], U32, f"h_c{h}_{g}") for g in range(2)] for h in range(2)]
         h_s = [[own([P, HALF], U8, f"h_s{h}_{g}") for g in range(2)] for h in range(2)]
         picked_x0 = own([P, J], F32, "picked_x0")
         picked_x = {(h, 0): picked_x0[:, HALF * h : HALF * (h + 1)] for h in range(2)}
@@ -75,20 +80,9 @@ def tile_list_xcross_none_kernel(
         wb_w = placed([P, 2, N // 2], I32, "wb_w", 24 * KB)
         up_raw = [placed([P, 4, N], F32, f"up_raw{g}", at * KB) for g, at in enumerate((26, 42))]
         x = [placed([P, T], F32, f"x{c}", at * KB) for c, at in enumerate((12, 34, 50, 58))]
-        dn_s_raw = placed([P, 2, R // 4], I32, "dn_s_raw", 68 * KB)
-        tab_parted = placed([P, 2 * J], U16, "tab_parted", 68 * KB)
-        h_bf = [
-            [placed([P, HALF, 4], BF16, f"h_bf0_{g}", (72 + 4 * g) * KB) for g in range(2)],
-            [own([P, HALF, 4], BF16, f"h_bf1_{g}") for g in range(2)],
-        ]
-        up_c = [placed([P, N], U32, f"up_c{g}", (72 + 4 * g) * KB) for g in range(2)]
-        h_c = [
-            [placed([P, HALF], U32, f"h_c0_{g}", at * KB) for g, at in enumerate((26, 42))],
-            [own([P, HALF], U32, f"h_c1_{g}") for g in range(2)],
-        ]
 
-        nc.gpsimd.memset(bias_rows[:], 0.0)
         nc.gpsimd.memset(tab_s[:].bitcast(I32), 0)
+        nc.gpsimd.memset(bias_rows[:], 0.0)
         nc.vector.memset(zeros[:, 0 : R // 2], 0)
         nc.vector.tensor_copy(dn_s_raw[:].rearrange("p a c -> p (a c)"), zeros[:, 0 : R // 2])
         nc.vector.memset(tab_plane[1][:].bitcast(I32), 0)
@@ -235,9 +229,9 @@ def tile_list_xcross_none_kernel(
         load_x(0)
         gather_scales(0, QUARTER)
         gather_scales(QUARTER, J)
-        order_dn_scales()
         gather_words(0)
         part_words(0)
+        order_dn_scales()
         order_dn(0)
         order_dn(1)
         nc.sync.dma_start(wb_w[:], wb_words.bitcast(I32).rearrange("a p c -> p a c"))
@@ -283,12 +277,16 @@ def tile_list_xcross_none_kernel(
         quantise_h(1, 1)
         finish(acc0[3], 0, 3)
 
-        acc1 = [ps_y.tile([P, HALF], F32, name="acc") for c in range(4)]
-        for c in range(4):
+        closing = (3, 0, 1, 2)
+        acc1 = {c: ps_h.tile([P, HALF], F32, name="bank") for c in closing}
+        for c in closing[:3]:
             y_from_wb(acc1[c], 1, c)
             y_from_up(acc1[c], 1, c, 0)
-        for c in (3, 0, 1, 2):
+        for c in closing[:3]:
             y_from_up(acc1[c], 1, c, 1)
+        y_from_wb(acc1[2], 1, 2)
+        for g in range(2):
+            y_from_up(acc1[2], 1, 2, g)
         empty_y(acc1[3], 1, 3)
         finish(acc1[0], 1, 0)
         finish(acc1[3], 1, 3)

@@ -25,7 +25,7 @@ PER_COLUMN = 16
 PLANE_GAP = 16
 KB = 1024
 FUSED = ((0, 1), (0, 2), (0, 3), (1, 3))
-PIECES = ((0, QUARTER), (QUARTER, HALF), (HALF, J))
+PIECES = ((0, QUARTER), (QUARTER, J))
 
 
 def tile_list_xcross_none_kernel(
@@ -74,8 +74,7 @@ def tile_list_xcross_none_kernel(
         first_picked = placed([P, 42 * KB // 4], U32, "first_picked", 24 * KB)
         picked_w = [
             first_picked[:, 0:QUARTER],
-            placed([P, QUARTER], U32, "picked_w1", 8 * KB)[:],
-            placed([P, HALF], U32, "picked_w2", 9 * KB)[:],
+            placed([P, J - QUARTER], U32, "picked_w1", 8 * KB)[:],
         ]
         wb_w = placed([P, 2, N // 2], I32, "wb_w", 24 * KB)
         up_raw = [placed([P, 4, N], F32, f"up_raw{g}", at * KB) for g, at in enumerate((26, 42))]
@@ -164,7 +163,10 @@ def tile_list_xcross_none_kernel(
                         stop=(a == 1),
                         **table_operand(h, a, cols),
                     )
-            nc.scalar.copy(h_bf[h][g][:, cols, 2 * pair : 2 * pair + 2], bank[:].rearrange("p e j -> p j e"))
+            nc.scalar.copy(
+                h_bf[h][g][:, cols, 2 * pair : 2 * pair + 2].rearrange("p (c i) e -> p c e i", i=2),
+                bank[:].rearrange("p e (c i) -> p c e i", i=2),
+            )
 
         def quantise_h(h, g):
             nc.vector.quantize_mx(
@@ -240,9 +242,7 @@ def tile_list_xcross_none_kernel(
         for c in range(1, 4):
             load_x(c)
         gather_words(1)
-        gather_words(2)
         part_words(1)
-        part_words(2)
         nc.vector.tensor_copy(picked_x0[:], x[0][:].indirect(entries[:]))
         cast_up(0)
 
@@ -269,24 +269,23 @@ def tile_list_xcross_none_kernel(
         gather_x(1, 2)
         h_bank(1, 1, 0, 0)
         quantise_h(1, 0)
-        for c in range(1, 4):
-            empty_y(acc0[c], 0, c)
-            h_bank(1, 1, c // 2, c % 2)
+        empty_y(acc0[1], 0, 1)
+        h_bank(1, 1, 0, 1)
+        empty_y(acc0[2], 0, 2)
+        h_bank(1, 1, 1, 0)
+        h_bank(1, 1, 1, 1)
+        empty_y(acc0[3], 0, 3)
         finish(acc0[1], 0, 1)
         finish(acc0[2], 0, 2)
         quantise_h(1, 1)
         finish(acc0[3], 0, 3)
 
-        closing = (3, 0, 1, 2)
-        acc1 = {c: ps_h.tile([P, HALF], F32, name="bank") for c in closing}
-        for c in closing[:3]:
+        acc1 = [ps_y.tile([P, HALF], F32, name="acc") for c in range(3)] + [ps_h.tile([P, HALF], F32, name="bank")]
+        for c in range(4):
             y_from_wb(acc1[c], 1, c)
             y_from_up(acc1[c], 1, c, 0)
-        for c in closing[:3]:
+        for c in (3, 0, 1, 2):
             y_from_up(acc1[c], 1, c, 1)
-        y_from_wb(acc1[2], 1, 2)
-        for g in range(2):
-            y_from_up(acc1[2], 1, 2, g)
         empty_y(acc1[3], 1, 3)
         finish(acc1[0], 1, 0)
         finish(acc1[3], 1, 3)

@@ -54,6 +54,7 @@ def tile_list_xcross_none_kernel(
         dn_s_raw = own([P, 2, R // 4], I32, "dn_s_raw")
         tab_parted = own([P, 2 * J], U16, "tab_parted")
         wb_s = own([P, 2, N // 4], I32, "wb_s")
+        zeros_wb = own([P, N // 2], I32, "zeros_wb")
         up_bf = [own([P, N, 4], BF16, f"up_bf{g}") for g in range(2)]
         up_s = [own([P, N], U8, f"up_s{g}") for g in range(2)]
         up_c = [own([P, N], U32, f"up_c{g}") for g in range(2)]
@@ -71,10 +72,10 @@ def tile_list_xcross_none_kernel(
         tab_w = placed([P, T], U32, "tab_w", 0)
         dn_w_raw = placed([P, 2, R // 2], I32, "dn_w_raw", 8 * KB)
         ident = placed([P, P], F32, "ident", 20 * KB)
-        first_picked = placed([P, 42 * KB // 4], U32, "first_picked", 24 * KB)
+        first_picked = placed([P, 45 * KB // 4], U32, "first_picked", 24 * KB)
         picked_w = [
             first_picked[:, 0:QUARTER],
-            placed([P, J - QUARTER], U32, "picked_w1", 8 * KB)[:],
+            placed([P, J - QUARTER], U32, "picked_w1", 66 * KB)[:],
         ]
         wb_w = placed([P, 2, N // 2], I32, "wb_w", 24 * KB)
         up_raw = [placed([P, 4, N], F32, f"up_raw{g}", at * KB) for g, at in enumerate((26, 42))]
@@ -85,7 +86,8 @@ def tile_list_xcross_none_kernel(
         nc.vector.memset(zeros[:, 0 : R // 2], 0)
         nc.vector.tensor_copy(dn_s_raw[:].rearrange("p a c -> p (a c)"), zeros[:, 0 : R // 2])
         nc.vector.memset(tab_plane[1][:].bitcast(I32), 0)
-        nc.vector.memset(wb_s[:], 0)
+        nc.vector.memset(zeros_wb[:], 0)
+        nc.scalar.copy(wb_s[:].rearrange("p a c -> p (a c)").bitcast(U32), zeros_wb[:].bitcast(U32))
         make_identity(nc, ident[:])
 
         nc.sync.dma_start(entries[:], offs)
@@ -101,6 +103,7 @@ def tile_list_xcross_none_kernel(
 
         load_planes(nc.sync, dn_s_raw, dn_scales)
         nc.sync.dma_start(dn_w_raw[:], dn_words.bitcast(I32).rearrange("a p c -> p a c"))
+        nc.gpsimd.dma_start(bias_rows[0:4, :], b.rearrange("(c p) -> c p", p=P))
         load_planes(nc.gpsimd, wb_s, wb_scales)
 
         up_src = upw.rearrange("(g u t i) n -> g t u i n", g=2, t=4, i=8)
@@ -132,15 +135,15 @@ def tile_list_xcross_none_kernel(
             nc.vector.tensor_copy(parted, picked_w[i].bitcast(U16).rearrange("p (j a) -> p a j", a=2))
 
         def order_dn(g):
-            nc.vector.tensor_copy(
-                dn_w[g][:].rearrange("p a (t u w) -> p a t u w", t=4, w=4),
-                dn_w_raw[:, :, 256 * g : 256 * (g + 1)].rearrange("p a (u t w) -> p a t u w", t=4, w=4),
+            nc.scalar.copy(
+                dn_w[g][:].bitcast(U32).rearrange("p a (t u w) -> p a t u w", t=4, w=4),
+                dn_w_raw[:, :, 256 * g : 256 * (g + 1)].bitcast(U32).rearrange("p a (u t w) -> p a t u w", t=4, w=4),
             )
 
         def order_dn_scales():
-            nc.vector.tensor_copy(
-                dn_s[:].rearrange("p a g (t u w) -> p (a g) t u w", t=4, w=2),
-                dn_s_raw[:].rearrange("p a (g u t w) -> p (a g) t u w", g=2, t=4, w=2),
+            nc.scalar.copy(
+                dn_s[:].bitcast(U32).rearrange("p a g (t u w) -> p (a g) t u w", t=4, w=2),
+                dn_s_raw[:].bitcast(U32).rearrange("p a (g u t w) -> p (a g) t u w", g=2, t=4, w=2),
             )
 
         def table_operand(h, a, cols):
@@ -223,7 +226,6 @@ def tile_list_xcross_none_kernel(
                 )
             nc.sync.dma_start(out[P * c : P * (c + 1), cols], done)
 
-        nc.scalar.dma_start(bias_rows[0:4, :], b.rearrange("(c p) -> c p", p=P))
         turned = ps_h.tile([P, P], F32, name="bank")
         nc.tensor.transpose(turned[:], bias_rows[:], ident[:])
         nc.scalar.activation(bias_plus_1[:], turned[:, 0:4], IDENTITY, bias=1.0)

from contextlib import ExitStack

import concourse.mybir as mybir
from concourse.masks import make_identity

K, R, N, T, J = 1024, 1024, 512, 2048, 1024
FLOPS = 2 * J * (K * R + K * N + R * N)

F32 = mybir.dt.float32
BF16 = mybir.dt.bfloat16
I32 = mybir.dt.int32
U32 = mybir.dt.uint32
U16 = mybir.dt.uint16
U8 = mybir.dt.uint8
FP8X4 = mybir.dt.float8_e4m3fn_x4
FP4X4 = mybir.dt.float4_e2m1fn_x4
ADD = mybir.AluOpType.add
MULT = mybir.AluOpType.mult
IDENTITY = mybir.ActivationFunctionType.Identity

P = 128
HALF = J // 2
QUARTER = J // 4
PER_COLUMN = 16
PLANE_GAP = 16
KB = 1024
FUSED = ((0, 1), (0, 2), (0, 3), (1, 3))
PIECES = ((0, QUARTER), (QUARTER, J))


def tile_list_xcross_none_kernel(
    tc, tab_words, tab_scales, wb_words, wb_scales, dn_words, dn_scales, upw, x0T, b, offs, out
):
    nc = tc.nc
    with ExitStack() as ctx:
        keep = ctx.enter_context(tc.tile_pool(name="keep", bufs=1))
        shared = ctx.enter_context(tc.tile_pool(name="shared", bufs=1))
        ps_h = ctx.enter_context(tc.psum_pool(name="ps_h", bufs=4))
        ps_y = ctx.enter_context(tc.psum_pool(name="ps_y", bufs=4))

        def own(shape, dtype, name):
            return keep.tile(shape, dtype, name=name, align_bytes=64)

        def placed(shape, dtype, name, offset):
            return shared.tile(shape, dtype, name=name, align_bytes=64, offset=offset)

        entries = keep.tile([P, J // PER_COLUMN], U16, name="entries")
        bias_rows = own([P, P], F32, "bias_rows")
        bias_plus_1 = own([P, 4], F32, "bias_plus_1")
        tab_s = own([P, T], U8, "tab_s")
        tab_plane = [own([P, J], U8, f"tab_plane{a}") for a in range(2)]
        dn_w = [own([P, 2, 256], I32, f"dn_w{g}") for g in range(2)]
        dn_s = own([P, 2, 2, 128], I32, "dn_s")
        dn_s_raw = own([P, 2, R // 4], I32, "dn_s_raw")
        tab_parted = own([P, 2 * J], U16, "tab_parted")
        wb_s = own([P, 2, N // 4], I32, "wb_s")
        zeros_wb = own([P, N // 2], I32, "zeros_wb")
        up_bf = [own([P, N, 4], BF16, f"up_bf{g}") for g in range(2)]
        up_s = [own([P, N], U8, f"up_s{g}") for g in range(2)]
        up_c = [own([P, N], U32, f"up_c{g}") for g in range(2)]
        h_bf = [[own([P, HALF, 4], BF16, f"h_bf{h}_{g}") for g in range(2)] for h in range(2)]
        h_c = [[own([P, HALF], U32, f"h_c{h}_{g}") for g in range(2)] for h in range(2)]
        h_s = [[own([P, HALF], U8, f"h_s{h}_{g}") for g in range(2)] for h in range(2)]
        picked_x0 = own([P, J], F32, "picked_x0")
        picked_x = {(h, 0): picked_x0[:, HALF * h : HALF * (h + 1)] for h in range(2)}
        for c in (1, 2):
            picked_x[1, c] = own([P, HALF], F32, f"picked_x{c}")[:]
        y_sb = {(h, c): own([P, HALF], F32, f"y_sb{h}_{c}") for h, c in FUSED}
        result = [[own([P, HALF], F32, f"result{h}_{c}") for c in range(4)] for h in range(2)]

        zeros = placed([P, (20 * KB + 4 * P) // 4], I32, "zeros", 0)
        tab_w = placed([P, T], U32, "tab_w", 0)
        dn_w_raw = placed([P, 2, R // 2], I32, "dn_w_raw", 8 * KB)
        ident = placed([P, P], F32, "ident", 20 * KB)
        first_picked = placed([P, 45 * KB // 4], U32, "first_picked", 24 * KB)
        picked_w = [
            first_picked[:, 0:QUARTER],
            placed([P, J - QUARTER], U32, "picked_w1", 66 * KB)[:],
        ]
        wb_w = placed([P, 2, N // 2], I32, "wb_w", 24 * KB)
        up_raw = [placed([P, 4, N], F32, f"up_raw{g}", at * KB) for g, at in enumerate((26, 42))]
        x = [placed([P, T], F32, f"x{c}", at * KB) for c, at in enumerate((12, 34, 50, 58))]

        nc.gpsimd.memset(tab_s[:].bitcast(I32), 0)
        nc.gpsimd.memset(bias_rows[:], 0.0)
        nc.vector.memset(zeros[:, 0 : R // 2], 0)
        nc.vector.tensor_copy(dn_s_raw[:].rearrange("p a c -> p (a c)"), zeros[:, 0 : R // 2])
        nc.vector.memset(tab_plane[1][:].bitcast(I32), 0)
        nc.vector.memset(zeros_wb[:], 0)
        nc.scalar.copy(wb_s[:].rearrange("p a c -> p (a c)").bitcast(U32), zeros_wb[:].bitcast(U32))
        make_identity(nc, ident[:])

        nc.sync.dma_start(entries[:], offs)
        tab_s_src = tab_scales.bitcast(I32).rearrange("a (q m) c -> m q a c", m=4)
        for m in range(4):
            nc.sync.dma_start(tab_s[:].bitcast(I32)[m:P:PLANE_GAP, :], tab_s_src[m])
        nc.sync.dma_start(tab_w[:].bitcast(I32), tab_words[0].rearrange("p t b -> p (t b)").bitcast(I32))

        def load_planes(queue, planes, scales):
            src = scales.bitcast(I32).rearrange("a (q m) c -> m q a c", m=4)
            for m in range(4):
                queue.dma_start(planes[m:P:32], src[m])

        load_planes(nc.sync, dn_s_raw, dn_scales)
        nc.sync.dma_start(dn_w_raw[:], dn_words.bitcast(I32).rearrange("a p c -> p a c"))
        nc.gpsimd.dma_start(bias_rows[0:4, :], b.rearrange("(c p) -> c p", p=P))
        load_planes(nc.gpsimd, wb_s, wb_scales)

        up_src = upw.rearrange("(g u t i) n -> g t u i n", g=2, t=4, i=8)

        def load_up(g):
            for t in range(4):
                nc.sync.dma_start(up_raw[g][:, t, :], up_src[g][t])

        def load_x(c):
            nc.sync.dma_start(x[c][:], x0T[P * c : P * (c + 1), :])

        def listed(lo, hi):
            return entries[:, lo // PER_COLUMN : hi // PER_COLUMN]

        def gather_scales(lo, hi):
            nc.vector.tensor_copy(tab_plane[0][:, lo:hi], tab_s[:].indirect(listed(lo, hi)))
            words = slice(lo // 4, hi // 4)
            nc.scalar.dma_start(
                tab_plane[1][:].bitcast(I32)[0 : P - PLANE_GAP, words], tab_plane[0][:].bitcast(I32)[PLANE_GAP:P, words]
            )

        def gather_words(i):
            lo, hi = PIECES[i]
            nc.vector.tensor_copy(picked_w[i], tab_w[:].indirect(listed(lo, hi)))

        def part_words(i):
            lo, hi = PIECES[i]
            parted = tab_parted[:].rearrange("p (a j) -> p a j", a=2)[:, :, lo:hi]
            nc.vector.tensor_copy(parted, picked_w[i].bitcast(U16).rearrange("p (j a) -> p a j", a=2))

        def order_dn(g):
            nc.scalar.copy(
                dn_w[g][:].bitcast(U32).rearrange("p a (t u w) -> p a t u w", t=4, w=4),
                dn_w_raw[:, :, 256 * g : 256 * (g + 1)].bitcast(U32).rearrange("p a (u t w) -> p a t u w", t=4, w=4),
            )

        def order_dn_scales():
            nc.scalar.copy(
                dn_s[:].bitcast(U32).rearrange("p a g (t u w) -> p (a g) t u w", t=4, w=2),
                dn_s_raw[:].bitcast(U32).rearrange("p a (g u t w) -> p (a g) t u w", g=2, t=4, w=2),
            )

        def table_operand(h, a, cols):
            return dict(
                rhs=tab_parted[:, J * a + HALF * h : J * a + HALF * (h + 1)][:, cols].bitcast(FP4X4),
                rhs_scale=tab_plane[a][:, HALF * h : HALF * (h + 1)][:, cols],
            )

        def h_bank(h, g, q, pair):
            bank = ps_h.tile([P, 2, QUARTER], F32, name="bank")
            cols = slice(QUARTER * q, QUARTER * (q + 1))
            for e in range(2):
                t = 2 * pair + e
                for a in range(2):
                    nc.tensor.matmul_mx(
                        out=bank[:, e, :],
                        lhsT=dn_w[g][:, a, 64 * t : 64 * (t + 1)].bitcast(FP4X4),
                        lhsT_scale=dn_s[:, a, g, 32 * t : 32 * (t + 1)].bitcast(U8),
                        start=(a == 0),
                        stop=(a == 1),
                        **table_operand(h, a, cols),
                    )
            nc.scalar.copy(
                h_bf[h][g][:, cols, 2 * pair : 2 * pair + 2].rearrange("p (c i) e -> p c e i", i=2),
                bank[:].rearrange("p e (c i) -> p c e i", i=2),
            )

        def quantise_h(h, g):
            nc.vector.quantize_mx(
                out=h_c[h][g][:].bitcast(FP8X4), scales=h_s[h][g][:], in_=h_bf[h][g][:].rearrange("p j t -> p (j t)")
            )

        def cast_up(g):
            nc.vector.tensor_copy(
                up_bf[g][:].rearrange("p (c i) t -> p c t i", i=4), up_raw[g][:].rearrange("p t (c i) -> p c t i", i=4)
            )

        def quantise_up(g):
            nc.vector.quantize_mx(
                out=up_c[g][:].bitcast(FP8X4), scales=up_s[g][:], in_=up_bf[g][:].rearrange("p n t -> p (n t)")
            )

        def y_from_wb(acc, h, c):
            for a in range(2):
                nc.tensor.matmul_mx(
                    out=acc[:],
                    lhsT=wb_w[:, a, 64 * c : 64 * (c + 1)].bitcast(FP4X4),
                    lhsT_scale=wb_s[:, a, 32 * c : 32 * (c + 1)].bitcast(U8),
                    start=(a == 0),
                    stop=False,
                    **table_operand(h, a, slice(0, HALF)),
                )

        def y_from_up(acc, h, c, g):
            cols = slice(P * c, P * (c + 1))
            nc.tensor.matmul_mx(
                out=acc[:],
                lhsT=up_c[g][:, cols].bitcast(FP8X4),
                lhsT_scale=up_s[g][:, cols],
                rhs=h_c[h][g][:].bitcast(FP8X4),
                rhs_scale=h_s[h][g][:],
                start=False,
                stop=(g == 1),
            )

        def gather_x(h, c):
            nc.vector.tensor_copy(picked_x[h, c], x[c][:].indirect(listed(HALF * h, HALF * (h + 1))))

        def empty_y(acc, h, c):
            nc.scalar.activation(y_sb[h, c][:], acc[:], IDENTITY, bias=bias_plus_1[:, c : c + 1])

        def finish(acc, h, c, lo=0, hi=HALF):
            done = result[h][c][:, lo:hi]
            cols = slice(HALF * h + lo, HALF * h + hi)
            if (h, c) in FUSED:
                nc.vector.tensor_tensor(done, x[c][:].indirect(listed(cols.start, cols.stop)), y_sb[h, c][:, lo:hi], MULT)
            else:
                nc.vector.scalar_tensor_tensor(
                    done, acc[:, lo:hi], bias_plus_1[:, c : c + 1], picked_x[h, c][:, lo:hi], ADD, MULT
                )
            nc.sync.dma_start(out[P * c : P * (c + 1), cols], done)

        turned = ps_h.tile([P, P], F32, name="bank")
        nc.tensor.transpose(turned[:], bias_rows[:], ident[:])
        nc.scalar.activation(bias_plus_1[:], turned[:, 0:4], IDENTITY, bias=1.0)

        load_x(0)
        gather_scales(0, QUARTER)
        gather_scales(QUARTER, J)
        gather_words(0)
        part_words(0)
        order_dn_scales()
        order_dn(0)
        order_dn(1)
        nc.sync.dma_start(wb_w[:], wb_words.bitcast(I32).rearrange("a p c -> p a c"))
        load_up(0)
        load_up(1)
        for c in range(1, 4):
            load_x(c)
        gather_words(1)
        part_words(1)
        nc.vector.tensor_copy(picked_x0[:], x[0][:].indirect(entries[:]))
        cast_up(0)

        acc0 = [ps_y.tile([P, HALF], F32, name="acc") for c in range(4)]
        for q in range(2):
            for g in range(2):
                for pair in range(2):
                    h_bank(0, g, q, pair)
                    if q == 1:
                        y_from_wb(acc0[2 * g + pair], 0, 2 * g + pair)
        quantise_h(0, 0)
        quantise_up(0)
        cast_up(1)
        quantise_h(0, 1)
        quantise_up(1)
        gather_x(1, 1)

        for q in range(2):
            for pair in range(2):
                h_bank(1, 0, q, pair)
            for c in range(4):
                y_from_up(acc0[c], 0, c, q)
        finish(acc0[0], 0, 0)
        gather_x(1, 2)
        h_bank(1, 1, 0, 0)
        quantise_h(1, 0)
        empty_y(acc0[1], 0, 1)
        h_bank(1, 1, 0, 1)
        empty_y(acc0[2], 0, 2)
        h_bank(1, 1, 1, 0)
        h_bank(1, 1, 1, 1)
        empty_y(acc0[3], 0, 3)
        finish(acc0[1], 0, 1)
        finish(acc0[2], 0, 2)
        quantise_h(1, 1)
        finish(acc0[3], 0, 3)

        acc1 = [ps_y.tile([P, HALF], F32, name="acc") for c in range(3)] + [ps_h.tile([P, HALF], F32, name="bank")]
        for c in range(4):
            y_from_wb(acc1[c], 1, c)
            y_from_up(acc1[c], 1, c, 0)
        for c in (3, 0, 1, 2):
            y_from_up(acc1[c], 1, c, 1)
        empty_y(acc1[3], 1, 3)
        finish(acc1[0], 1, 0)
        finish(acc1[3], 1, 3)
        finish(acc1[1], 1, 1)
        finish(acc1[2], 1, 2, 0, QUARTER)
        finish(acc1[2], 1, 2, QUARTER, HALF)
